import numpy as np
import ml_dtypes


def mxq(x, axis, fmt="e4m3"):
    dtype, down = {"e4m3": (ml_dtypes.float8_e4m3fn, 7), "e5m2": (ml_dtypes.float8_e5m2, 14)}[fmt]
    v = np.moveaxis(np.asarray(x, np.float32).astype(ml_dtypes.bfloat16).astype(np.float64), axis, -1)
    blocks = v.reshape(v.shape[:-1] + (-1, 32))
    amax = np.abs(blocks).max(-1, keepdims=True)
    byte = np.maximum(np.where(amax > 0, np.frexp(amax)[1] - 1 + 127, 0) - down, 1)
    scale = np.exp2(byte - 127.0)
    codes = (blocks / scale).astype(np.float32).astype(dtype).astype(np.float64)
    return np.moveaxis((codes * scale).reshape(v.shape), -1, axis)


WIDE = False


def mx_kscale(k):
    if not WIDE:
        return np.ones(k)
    levels = np.array([10, -10, 5, -5, 0])
    if k % 512:
        return np.exp2(np.random.permutation(np.resize(levels, k // 32))).repeat(32)
    a = np.empty((k // 512, 16))
    for p in range(k // 512):
        a[p, :8] = np.random.permutation(np.resize(levels, 8))
        for g in range(8):
            far = levels[np.abs(levels - a[p, g]) >= 10]
            a[p, g + 8] = far[np.random.randint(len(far))]
    return np.exp2(a.ravel()).repeat(32)


def f64(x):
    return np.asarray(x).astype(np.float64)


def striped(idx):
    return np.tile(idx.reshape(-1, 16).T, (8, 1)).astype(np.uint16)


def unstriped(offs):
    return offs[:16].T.reshape(-1).astype(np.int64)


E2M1 = np.array([0.0, 0.5, 1.0, 1.5, 2.0, 3.0, 4.0, 6.0, -0.0, -0.5, -1.0, -1.5, -2.0, -3.0, -4.0, -6.0])


def pack_weight(w, fmt):
    k, n = w.shape
    w = f64(np.asarray(w, np.float32).astype(ml_dtypes.bfloat16)).reshape(k // 32, 32, n)
    amax = np.abs(w).max(1)
    if fmt == "e4m3":
        byte = np.frexp(amax)[1] - 1 + 127 - 7
    else:
        mant, ex = np.frexp(amax / 6.0)
        byte = np.where(mant > 0.5, ex, ex - 1) + 127
    byte = np.clip(np.where(amax > 0, byte, 1), 1, 254)
    scaled = (w * np.exp2(127.0 - byte)[:, None, :]).reshape(k, n).astype(np.float32)
    by_word = np.ascontiguousarray(scaled.reshape(k // 512, 128, 4, n).transpose(0, 1, 3, 2))
    if fmt == "e4m3":
        words = by_word.astype(ml_dtypes.float8_e4m3fn).view(np.uint8)
    else:
        c = by_word.astype(ml_dtypes.float4_e2m1fn).view(np.uint8) & 0xF
        words = (c[..., 0::2] | (c[..., 1::2] << 4)).reshape(k // 512, 128, 2 * n)
    return np.ascontiguousarray(words), np.ascontiguousarray(byte.astype(np.uint8).reshape(k // 512, 16, n))


def unpack_weight(words, scales, fmt):
    g, _, n = scales.shape
    words = np.ascontiguousarray(words).reshape(g, 128, n, -1)
    if fmt == "e4m3":
        vals = words.view(ml_dtypes.float8_e4m3fn).astype(np.float64)
    else:
        nib = np.empty((g, 128, n, 4), np.uint8)
        nib[..., 0::2] = words & 0xF
        nib[..., 1::2] = words >> 4
        vals = E2M1[nib]
    vals = vals * np.repeat(np.exp2(scales.astype(np.float64) - 127.0), 8, axis=1)[..., None]
    return vals.transpose(0, 1, 3, 2).reshape(g * 512, n)


def gelu(v):
    return 0.5 * v * (1.0 + np.tanh(np.sqrt(2.0 / np.pi) * (v + 0.044715 * v**3)))


def bf(x):
    return np.asarray(x, np.float32).astype(ml_dtypes.bfloat16)

def planes(Y):
    n, m = Y.shape
    b = f64(bf(Y)).reshape(n // 32, 32, m)
    amax = np.abs(b).max(1)
    byte = np.clip(np.where(amax > 0, np.frexp(amax)[1] - 1 + 127 - 7, 1), 1, 254)
    codes = (b * np.exp2(127.0 - byte)[:, None, :]).reshape(n, m).astype(np.float32).astype(ml_dtypes.float8_e4m3fn).view(np.uint8)
    words = codes.reshape(n // 512, 128, 4, m).transpose(0, 1, 3, 2)
    return np.ascontiguousarray(words), np.ascontiguousarray(byte.astype(np.uint8).reshape(n // 512, 16, m))


K, T, S, H, N = 1024, 4096, 1024, 1024, 512

def setup_inputs():
    n = np.random.standard_normal
    s = mx_kscale(K)[:, None]
    u = mx_kscale(H)[:, None]
    gain = np.exp(0.8 * n(N))
    tab_words, tab_scales = pack_weight((0.6 + n((K, T))) * s, "e4m3")
    ws = (0.05 + n((K, H)) / np.sqrt(K)) if K == 1 else (0.05 + n((K, H))) / np.sqrt(K)
    we = (0.05 + n((K, H))) / np.sqrt(K)
    we_words, we_scales = pack_weight(we / s * u.T, "e2m1")
    wi_words, wi_scales = pack_weight(n((H, N)) / np.sqrt(H) * gain[None, :] / u, "e4m3")
    return {
        "tab_words": tab_words, "tab_scales": tab_scales,
        "offs": striped(np.random.permutation(T)[:S]),
        "ws": (ws / s * u.T).astype(np.float32),
        "we_words": we_words, "we_scales": we_scales,
        "wi_words": wi_words, "wi_scales": wi_scales,
        "b": (0.5 * n(N) * gain).astype(np.float32),
    }

def reference(tab_words, tab_scales, offs, ws, we_words, we_scales, wi_words, wi_scales, b):
    v = unpack_weight(tab_words, tab_scales, "e4m3")[:, unstriped(offs)]
    size = mxq(f64(ws), 0, "e4m3").T @ v
    energy = unpack_weight(we_words, we_scales, "e2m1").T @ v
    h = np.sqrt(np.maximum(size, 0.0) * np.maximum(energy, 0.0))
    y = (unpack_weight(wi_words, wi_scales, "e4m3").T @ mxq(h, 0, "e4m3")) + f64(b)[:, None]
    words, scales = planes(y)
    return y, words, scales

@@ -1,0 +1,253 @@
+from contextlib import ExitStack
+
+import concourse.mybir as mybir
+
+K, T, S, H, N = 1024, 4096, 1024, 1024, 512
+FLOPS = 2 * K * H * S * 2 + 2 * H * N * S
+
+F32 = mybir.dt.float32
+BF16 = mybir.dt.bfloat16
+I32 = mybir.dt.int32
+U32 = mybir.dt.uint32
+U16 = mybir.dt.uint16
+U8 = mybir.dt.uint8
+FP8X4 = mybir.dt.float8_e4m3fn_x4
+FP4X4 = mybir.dt.float4_e2m1fn_x4
+ACT = mybir.ActivationFunctionType
+ALU = mybir.AluOpType
+
+P = 128
+PASS = 512
+HALF = 512
+
+
+def tile_list_mixture_geomean_interactions_kernel(
+    tc, tab_words, tab_scales, offs, ws, we_words, we_scales, wi_words, wi_scales, b, out_0, out_1, out_2
+):
+    nc = tc.nc
+    with ExitStack() as ctx:
+        keep = ctx.enter_context(tc.tile_pool(name="keep", bufs=1))
+        ring = ctx.enter_context(tc.tile_pool(name="ring", bufs=2))
+        psum = ctx.enter_context(tc.psum_pool(name="psum", bufs=8))
+
+        def held(shape, dtype, name):
+            return keep.tile(shape, dtype, name=name, align_bytes=64)
+
+        offsets = keep.tile([P, S // 16], U16, name="offsets")
+        nc.sync.dma_start(offsets[:], offs)
+
+        tab_sc = held([P, T], U8, "tab_sc")
+        w_sc_raw = held([P, H + N], U8, "w_sc_raw")
+        planes = [held([P, S + H + N], U8, "planes%d" % a) for a in range(2)]
+        rows = planes[0]
+        warm = held([P, 16], F32, "warm")
+        warm_out = held([P, 16], F32, "warm_out")
+        nc.sync.dma_start(tab_sc[0:32, :].bitcast(I32), tab_scales.rearrange("a q t -> (a q) t").bitcast(I32))
+        nc.sync.dma_start(w_sc_raw[0:32, 0:H].bitcast(I32), we_scales.rearrange("a q c -> (a q) c").bitcast(I32))
+        nc.sync.dma_start(w_sc_raw[0:32, H:].bitcast(I32), wi_scales.rearrange("a q c -> (a q) c").bitcast(I32))
+        nc.vector.memset(warm[:], 1.0)
+        for lo, hi in ((32, 64), (64, P)):
+            nc.vector.memset(w_sc_raw[lo:hi, :].bitcast(I32), 0)
+            nc.vector.memset(tab_sc[lo:hi, :].bitcast(I32), 0)
+        nc.vector.memset(planes[1][:].bitcast(I32), 0)
+        nc.scalar.activation(warm_out[:], warm[:], ACT.Sqrt)
+
+        we_raw = held([P, 2, PASS], I32, "we_raw")
+        nc.sync.dma_start(we_raw[:], we_words.rearrange("a p c -> p a c").bitcast(I32))
+        tab_w = []
+        for a, tag in enumerate(("first", "second")):
+            tab_w.append(keep.tile([P, T], I32, name="tab_w%d" % a, tag=tag, align_bytes=64))
+            nc.sync.dma_start(tab_w[a][:], tab_words[a].rearrange("p t i -> p (t i)").bitcast(I32))
+
+        picked_sc = held([P, S], U8, "picked_sc")
+        nc.vector.tensor_copy(
+            rows[:, S:].rearrange("p (g t m) -> p g m t", g=3, t=4),
+            w_sc_raw[:].rearrange("p (g m t) -> p g m t", g=3, t=4),
+        )
+        nc.vector.tensor_copy(picked_sc[:], tab_sc[:].indirect(offsets[:]))
+        nc.vector.tensor_copy(rows[:, 0:S].bitcast(I32), picked_sc[:].bitcast(I32))
+
+        for a in range(2):
+            for q in range(4):
+                r0 = 16 * a + 4 * q
+                if r0 > 0:
+                    eng = nc.gpsimd if (a, q) == (1, 3) else nc.sync
+                    eng.dma_start(planes[a][32 * q : 32 * q + 4, :].bitcast(I32), rows[r0 : r0 + 4, :].bitcast(I32))
+        v_sc = [planes[a][:, 0:S] for a in range(2)]
+        we_sc = [planes[a][:, S : S + H] for a in range(2)]
+        wi_sc = [planes[a][:, S + H :] for a in range(2)]
+
+        we_w = [keep.tile([P, 2 * H], U8, name="we_w%d" % a, tag="we_w%d" % a, align_bytes=64) for a in range(2)]
+        for a in range(2):
+            nc.vector.tensor_copy(
+                we_w[a][:].bitcast(U16).rearrange("p (g t m) -> p g m t", g=2, t=4),
+                we_raw[:, a, :].bitcast(U16).rearrange("p (g m t) -> p g m t", g=2, t=4),
+            )
+        v_w = {}
+        for a in range(2):
+            for jh in range(2):
+                v_w[a, jh] = held([P, HALF], U32, "v_w%d%d" % (a, jh))
+                cols = slice(jh * HALF // 16, (jh + 1) * HALF // 16)
+                nc.vector.tensor_copy(v_w[a, jh][:], tab_w[a][:].bitcast(U32).indirect(offsets[:, cols]))
+
+        ws_all = keep.tile([P, 2, 2, 4, PASS], F32, name="ws_all", tag="first", align_bytes=64)
+        ws_raw = {}
+        for g in range(2):
+            for a in range(2):
+                ws_raw[a, g] = ws_all[:, g, a, :, :]
+                block = ws[PASS * a : PASS * (a + 1), PASS * g : PASS * (g + 1)]
+                nc.sync.dma_start(ws_raw[a, g], block.rearrange("(p j) c -> p j c", j=4))
+        wi_raw = keep.tile([P, 2, PASS], I32, name="wi_raw", tag="second", align_bytes=64)
+        nc.sync.dma_start(wi_raw[:], wi_words.rearrange("a p c i -> p a (c i)").bitcast(I32))
+
+        ws_w, ws_sc = {}, {}
+
+        def quantise_ws(a, g, cast=nc.vector.tensor_copy):
+            grouped = ring.tile([P, 4 * PASS], BF16, name="ws_bf", tag="ws_bf", align_bytes=64)
+            cast(
+                grouped[:].rearrange("p (t m j) -> p m j t", t=4, j=4),
+                ws_raw[a, g].rearrange("p j (m t) -> p m j t", t=4),
+            )
+            ws_w[a, g] = held([P, PASS], U32, "ws_w%d%d" % (a, g))
+            ws_sc[a, g] = held([P, PASS], U8, "ws_sc%d%d" % (a, g))
+            nc.vector.quantize_mx(out=ws_w[a, g][:].bitcast(FP8X4), scales=ws_sc[a, g][:], in_=grouped[:])
+
+        pos_energy = {}
+
+        def energy(g, halves):
+            accs = {}
+            banks = [(jh, t) for jh in halves for t in range(4)]
+            if g == 0:
+                steps = [(a, bank) for a in range(2) for bank in banks]
+            else:
+                steps = [(a, bank) for bank in banks for a in range(2)]
+            for jh in halves:
+                pos_energy[g, jh] = held([P, 4, HALF], F32, "pos_energy%d%d" % (g, jh))
+            for a, (jh, t) in steps:
+                if a == 0:
+                    accs[jh, t] = psum.tile([P, HALF], F32, name="acc", tag="acc")
+                c0 = PASS * g + P * t
+                nc.tensor.matmul_mx(
+                    out=accs[jh, t][:],
+                    lhsT=we_w[a][:, 2 * c0 : 2 * (c0 + P)].bitcast(FP4X4),
+                    lhsT_scale=we_sc[a][:, c0 : c0 + P],
+                    rhs=v_w[a, jh][:].bitcast(FP8X4),
+                    rhs_scale=v_sc[a][:, jh * HALF : (jh + 1) * HALF],
+                    start=(a == 0),
+                    stop=(a == 1),
+                )
+                if a == 1:
+                    nc.scalar.activation(pos_energy[g, jh][:, t, :], accs[jh, t][:], ACT.Relu)
+
+        h_w, h_sc = {}, {}
+
+        def size(g, c0, width):
+            jh, lo = divmod(c0, HALF)
+            prod = ring.tile([P, 4, width], F32, name="prod", tag="prod", bufs=3, align_bytes=64)
+            per = HALF // width
+            for t0 in range(0, 4, per):
+                acc = psum.tile([P, per, width], F32, name="acc", tag="acc")
+                for t in range(t0, t0 + per):
+                    for a in (1, 0):
+                        nc.tensor.matmul_mx(
+                            out=acc[:, t - t0, :],
+                            lhsT=ws_w[a, g][:, P * t : P * (t + 1)].bitcast(FP8X4),
+                            lhsT_scale=ws_sc[a, g][:, P * t : P * (t + 1)],
+                            rhs=v_w[a, jh][:, lo : lo + width].bitcast(FP8X4),
+                            rhs_scale=v_sc[a][:, c0 : c0 + width],
+                            start=(a == 1),
+                            stop=(a == 0),
+                        )
+                nc.vector.scalar_tensor_tensor(
+                    out=prod[:, t0 : t0 + per, :],
+                    in0=acc[:],
+                    scalar=0.0,
+                    in1=pos_energy[g, jh][:, t0 : t0 + per, lo : lo + width],
+                    op0=ALU.max,
+                    op1=ALU.mult,
+                )
+            h_bf = ring.tile([P, 4 * width], BF16, name="h_bf", tag="h_bf", bufs=3, align_bytes=64)
+            nc.scalar.activation(
+                h_bf[:].rearrange("p (c i t) -> p c t i", i=4, t=4),
+                prod[:].rearrange("p t (c i) -> p c t i", i=4),
+                ACT.Sqrt,
+            )
+            h_w[g, c0] = held([P, width], U32, "h_w%d_%d" % (g, c0))
+            h_sc[g, c0] = held([P, width], U8, "h_sc%d_%d" % (g, c0))
+            nc.vector.quantize_mx(out=h_w[g, c0][:].bitcast(FP8X4), scales=h_sc[g, c0][:], in_=h_bf[:])
+
+        wi_w = held([P, 2, N], I32, "wi_w")
+
+        bias = []
+
+        def deal_wi():
+            bias.append(keep.tile([P, 4], F32, name="bias", tag="we_w1", align_bytes=64))
+            nc.sync.dma_start(bias[0][:], b.rearrange("(p t) -> p t", t=4))
+            nc.vector.tensor_copy(
+                wi_w[:].rearrange("p a (t m) -> p a m t", t=4), wi_raw[:].rearrange("p a (m t) -> p a m t", t=4)
+            )
+
+        y_sc = held([P, S], U8, "y_sc")
+        y_rows = out_0.rearrange("(p t) j -> p t j", t=4)
+        y_words = out_1[0].rearrange("p m i -> p (m i)").bitcast(I32)
+
+        ys = {}
+
+        def interactions(c0, width):
+            y = ys[c0] = held([P, 4, width], F32, "y%d" % c0)
+            for t0 in (0, 2):
+                acc = psum.tile([P, 2, width], F32, name="acc", tag="acc")
+                for t in (t0, t0 + 1):
+                    for g in (1, 0):
+                        nc.tensor.matmul_mx(
+                            out=acc[:, t - t0, :],
+                            lhsT=wi_w[:, g, P * t : P * (t + 1)].bitcast(FP8X4),
+                            lhsT_scale=wi_sc[g][:, P * t : P * (t + 1)],
+                            rhs=h_w[g, c0][:].bitcast(FP8X4),
+                            rhs_scale=h_sc[g, c0][:],
+                            start=(g == 1),
+                            stop=(g == 0),
+                        )
+                if t0 == 0:
+                    for t in (0, 1):
+                        nc.scalar.activation(y[:, t, :], acc[:, t, :], ACT.Identity, bias=bias[0][:, t : t + 1])
+                else:
+                    nc.vector.tensor_tensor(
+                        y[:, 2:4, :], acc[:], bias[0][:, 2:4].unsqueeze(2).to_broadcast([P, 2, width]), ALU.add
+                    )
+            nc.sync.dma_start(y_rows[:, :, c0 : c0 + width], y[:])
+
+        def out_planes(c0, width):
+            y_bf = ring.tile([P, 4 * width], BF16, name="y_bf", tag="y_bf", align_bytes=64)
+            nc.vector.tensor_copy(
+                y_bf[:].rearrange("p (c i t) -> p c t i", i=4, t=4),
+                ys[c0][:].rearrange("p t (c i) -> p c t i", i=4),
+            )
+            y_w = held([P, width], I32, "y_w%d" % c0)
+            nc.vector.quantize_mx(out=y_w[:].bitcast(FP8X4), scales=y_sc[:, c0 : c0 + width], in_=y_bf[:])
+            nc.sync.dma_start(y_words[:, c0 : c0 + width], y_w[:])
+
+        chunks = [(0,256),(256,256),(512,256),(768,256)]
+        energy(0, [0, 1])
+        quantise_ws(0, 0)
+        quantise_ws(1, 0)
+        energy(1, [0])
+        quantise_ws(0, 1)
+        quantise_ws(1, 1, nc.scalar.copy)
+        size(0, *chunks[0])
+        deal_wi()
+        size(1, *chunks[0])
+        size(0, *chunks[1])
+        size(1, *chunks[1])
+        interactions(*chunks[0])
+        energy(1, [1])
+        for i in range(2, len(chunks)):
+            size(0, *chunks[i])
+            size(1, *chunks[i])
+            interactions(*chunks[i - 1])
+        interactions(*chunks[-1])
+        for c in chunks:
+            out_planes(*c)
+        for q in range(4):
+            eng = nc.scalar if q % 2 else nc.sync
+            eng.dma_start(out_2[0, 4 * q : 4 * q + 4, :].bitcast(I32), y_sc[32 * q : 32 * q + 4, :].bitcast(I32))

@@ -60,18 +60,18 @@ def tile_list_mixture_geomean_interactions_kernel(
             nc.sync.dma_start(tab_w[a][:], tab_words[a].rearrange("p t i -> p (t i)").bitcast(I32))
 
         picked_sc = held([P, S], U8, "picked_sc")
+        nc.vector.tensor_copy(picked_sc[:], tab_sc[:].indirect(offsets[:]))
         nc.vector.tensor_copy(
             rows[:, S:].rearrange("p (g t m) -> p g m t", g=3, t=4),
             w_sc_raw[:].rearrange("p (g m t) -> p g m t", g=3, t=4),
         )
-        nc.vector.tensor_copy(picked_sc[:], tab_sc[:].indirect(offsets[:]))
         nc.vector.tensor_copy(rows[:, 0:S].bitcast(I32), picked_sc[:].bitcast(I32))
 
         for a in range(2):
             for q in range(4):
                 r0 = 16 * a + 4 * q
                 if r0 > 0:
-                    eng = nc.gpsimd if (a, q) == (1, 3) else nc.sync
+                    eng = nc.gpsimd if (a, q) == (1, 3) else nc.scalar
                     eng.dma_start(planes[a][32 * q : 32 * q + 4, :].bitcast(I32), rows[r0 : r0 + 4, :].bitcast(I32))
         v_sc = [planes[a][:, 0:S] for a in range(2)]
         we_sc = [planes[a][:, S : S + H] for a in range(2)]
@@ -208,9 +208,9 @@ def tile_list_mixture_geomean_interactions_kernel(
                             start=(g == 1),
                             stop=(g == 0),
                         )
-                if t0 == 0:
-                    for t in (0, 1):
-                        nc.scalar.activation(y[:, t, :], acc[:, t, :], ACT.Identity, bias=bias[0][:, t : t + 1])
+                if t0 == 0 or c0 < 512:
+                    for t in (t0, t0 + 1):
+                        nc.scalar.activation(y[:, t, :], acc[:, t - t0, :], ACT.Identity, bias=bias[0][:, t : t + 1])
                 else:
                     nc.vector.tensor_tensor(
                         y[:, 2:4, :], acc[:], bias[0][:, 2:4].unsqueeze(2).to_broadcast([P, 2, width]), ALU.add
@@ -233,7 +233,7 @@ def tile_list_mixture_geomean_interactions_kernel(
         quantise_ws(1, 0)
         energy(1, [0])
         quantise_ws(0, 1)
-        quantise_ws(1, 1, nc.scalar.copy)
+        quantise_ws(1, 1)
         size(0, *chunks[0])
         deal_wi()
         size(1, *chunks[0])

@@ -47,9 +47,9 @@ def tile_list_mixture_geomean_interactions_kernel(
         nc.sync.dma_start(w_sc_raw[0:32, H:].bitcast(I32), wi_scales.rearrange("a q c -> (a q) c").bitcast(I32))
         nc.vector.memset(warm[:], 1.0)
         for lo, hi in ((32, 64), (64, P)):
-            nc.vector.memset(w_sc_raw[lo:hi, :].bitcast(I32), 0)
             nc.vector.memset(tab_sc[lo:hi, :].bitcast(I32), 0)
-        nc.vector.memset(planes[1][:].bitcast(I32), 0)
+            nc.gpsimd.memset(w_sc_raw[lo:hi, :].bitcast(I32), 0)
+        nc.gpsimd.memset(planes[1][:].bitcast(I32), 0)
         nc.scalar.activation(warm_out[:], warm[:], ACT.Sqrt)
 
         we_raw = held([P, 2, PASS], I32, "we_raw")
@@ -59,11 +59,11 @@ def tile_list_mixture_geomean_interactions_kernel(
             tab_w.append(keep.tile([P, T], I32, name="tab_w%d" % a, tag=tag, align_bytes=64))
             nc.sync.dma_start(tab_w[a][:], tab_words[a].rearrange("p t i -> p (t i)").bitcast(I32))
 
-        picked_sc = held([P, S], U8, "picked_sc")
+        picked_sc = keep.tile([P, S], U8, name="picked_sc", tag="we_w0", align_bytes=64)
         nc.vector.tensor_copy(picked_sc[:], tab_sc[:].indirect(offsets[:]))
         nc.vector.tensor_copy(
-            rows[:, S:].rearrange("p (g t m) -> p g m t", g=3, t=4),
-            w_sc_raw[:].rearrange("p (g m t) -> p g m t", g=3, t=4),
+            rows[:, S:].rearrange("p (g t m) -> p g t m", g=3, t=4),
+            w_sc_raw[:].rearrange("p (g m t) -> p g t m", g=3, t=4),
         )
         nc.vector.tensor_copy(rows[:, 0:S].bitcast(I32), picked_sc[:].bitcast(I32))
 
@@ -77,12 +77,12 @@ def tile_list_mixture_geomean_interactions_kernel(
         we_sc = [planes[a][:, S : S + H] for a in range(2)]
         wi_sc = [planes[a][:, S + H :] for a in range(2)]
 
-        we_w = [keep.tile([P, 2 * H], U8, name="we_w%d" % a, tag="we_w%d" % a, align_bytes=64) for a in range(2)]
-        for a in range(2):
-            nc.vector.tensor_copy(
-                we_w[a][:].bitcast(U16).rearrange("p (g t m) -> p g m t", g=2, t=4),
-                we_raw[:, a, :].bitcast(U16).rearrange("p (g m t) -> p g m t", g=2, t=4),
-            )
+        we_all = keep.tile([P, 2, 2 * H], U8, name="we_all", tag="we_w0", align_bytes=64)
+        nc.vector.tensor_copy(
+            we_all[:].bitcast(U16).rearrange("p a (g t m) -> p (a g) t m", g=2, t=4),
+            we_raw[:].bitcast(U16).rearrange("p a (g m t) -> p (a g) t m", g=2, t=4),
+        )
+        we_w = [we_all[:, a, :] for a in range(2)]
         v_w = {}
         for a in range(2):
             for jh in range(2):
@@ -181,10 +181,11 @@ def tile_list_mixture_geomean_interactions_kernel(
         bias = []
 
         def deal_wi():
-            bias.append(keep.tile([P, 4], F32, name="bias", tag="we_w1", align_bytes=64))
+            bias.append(keep.tile([P, 4], F32, name="bias", tag="we_w0", align_bytes=64))
             nc.sync.dma_start(bias[0][:], b.rearrange("(p t) -> p t", t=4))
             nc.vector.tensor_copy(
-                wi_w[:].rearrange("p a (t m) -> p a m t", t=4), wi_raw[:].rearrange("p a (m t) -> p a m t", t=4)
+                wi_w[:].rearrange("p a (t o i) -> p a o t i", t=4, i=4),
+                wi_raw[:].rearrange("p a (o i t) -> p a o t i", t=4, i=4),
             )
 
         y_sc = held([P, S], U8, "y_sc")

@@ -27,7 +27,6 @@ def tile_list_mixture_geomean_interactions_kernel(
     nc = tc.nc
     with ExitStack() as ctx:
         keep = ctx.enter_context(tc.tile_pool(name="keep", bufs=1))
-        ring = ctx.enter_context(tc.tile_pool(name="ring", bufs=2))
         psum = ctx.enter_context(tc.psum_pool(name="psum", bufs=8))
 
         def held(shape, dtype, name):
@@ -102,15 +101,19 @@ def tile_list_mixture_geomean_interactions_kernel(
 
         ws_w, ws_sc = {}, {}
 
-        def quantise_ws(a, g, cast=nc.vector.tensor_copy):
-            grouped = ring.tile([P, 4 * PASS], BF16, name="ws_bf", tag="ws_bf", align_bytes=64)
-            cast(
-                grouped[:].rearrange("p (t m j) -> p m j t", t=4, j=4),
+        ws_bf = {}
+
+        def round_ws(a, g):
+            ws_bf[a, g] = held([P, 4 * PASS], BF16, "ws_bf%d%d" % (a, g))
+            nc.vector.tensor_copy(
+                ws_bf[a, g][:].rearrange("p (t m j) -> p m j t", t=4, j=4),
                 ws_raw[a, g].rearrange("p j (m t) -> p m j t", t=4),
             )
+
+        def quantise_ws(a, g):
             ws_w[a, g] = held([P, PASS], U32, "ws_w%d%d" % (a, g))
             ws_sc[a, g] = held([P, PASS], U8, "ws_sc%d%d" % (a, g))
-            nc.vector.quantize_mx(out=ws_w[a, g][:].bitcast(FP8X4), scales=ws_sc[a, g][:], in_=grouped[:])
+            nc.vector.quantize_mx(out=ws_w[a, g][:].bitcast(FP8X4), scales=ws_sc[a, g][:], in_=ws_bf[a, g][:])
 
         pos_energy = {}
 
@@ -139,11 +142,11 @@ def tile_list_mixture_geomean_interactions_kernel(
                 if a == 1:
                     nc.scalar.activation(pos_energy[g, jh][:, t, :], accs[jh, t][:], ACT.Relu)
 
-        h_w, h_sc = {}, {}
+        h_w, h_sc, prods, h_bfs = {}, {}, {}, {}
 
         def size(g, c0, width):
             jh, lo = divmod(c0, HALF)
-            prod = ring.tile([P, 4, width], F32, name="prod", tag="prod", bufs=3, align_bytes=64)
+            prod = prods[g, c0] = held([P, 4, width], F32, "prod%d_%d" % (g, c0))
             per = HALF // width
             for t0 in range(0, 4, per):
                 acc = psum.tile([P, per, width], F32, name="acc", tag="acc")
@@ -166,12 +169,18 @@ def tile_list_mixture_geomean_interactions_kernel(
                     op0=ALU.max,
                     op1=ALU.mult,
                 )
-            h_bf = ring.tile([P, 4 * width], BF16, name="h_bf", tag="h_bf", bufs=3, align_bytes=64)
+
+        def root(g, c0, width):
+            prod = prods[g, c0]
+            h_bf = h_bfs[g, c0] = held([P, 4 * width], BF16, "h_bf%d_%d" % (g, c0))
             nc.scalar.activation(
                 h_bf[:].rearrange("p (c i t) -> p c t i", i=4, t=4),
                 prod[:].rearrange("p t (c i) -> p c t i", i=4),
                 ACT.Sqrt,
             )
+
+        def quantise_h(g, c0, width):
+            h_bf = h_bfs[g, c0]
             h_w[g, c0] = held([P, width], U32, "h_w%d_%d" % (g, c0))
             h_sc[g, c0] = held([P, width], U8, "h_sc%d_%d" % (g, c0))
             nc.vector.quantize_mx(out=h_w[g, c0][:].bitcast(FP8X4), scales=h_sc[g, c0][:], in_=h_bf[:])
@@ -189,27 +198,31 @@ def tile_list_mixture_geomean_interactions_kernel(
             )
 
         y_sc = held([P, S], U8, "y_sc")
+        y_w = held([P, S], I32, "y_w")
         y_rows = out_0.rearrange("(p t) j -> p t j", t=4)
         y_words = out_1[0].rearrange("p m i -> p (m i)").bitcast(I32)
 
         ys = {}
 
-        def interactions(c0, width):
+        def interaction_pass(c0, width, t, g, acc):
+            nc.tensor.matmul_mx(
+                out=acc,
+                lhsT=wi_w[:, g, P * t : P * (t + 1)].bitcast(FP8X4),
+                lhsT_scale=wi_sc[g][:, P * t : P * (t + 1)],
+                rhs=h_w[g, c0][:].bitcast(FP8X4),
+                rhs_scale=h_sc[g, c0][:],
+                start=(g == 0),
+                stop=(g == 1),
+            )
+
+        def interactions(c0, width, shared=False):
             y = ys[c0] = held([P, 4, width], F32, "y%d" % c0)
             for t0 in (0, 2):
                 acc = psum.tile([P, 2, width], F32, name="acc", tag="acc")
                 for t in (t0, t0 + 1):
-                    for g in (1, 0):
-                        nc.tensor.matmul_mx(
-                            out=acc[:, t - t0, :],
-                            lhsT=wi_w[:, g, P * t : P * (t + 1)].bitcast(FP8X4),
-                            lhsT_scale=wi_sc[g][:, P * t : P * (t + 1)],
-                            rhs=h_w[g, c0][:].bitcast(FP8X4),
-                            rhs_scale=h_sc[g, c0][:],
-                            start=(g == 1),
-                            stop=(g == 0),
-                        )
-                if t0 == 0 or c0 < 512:
+                    for g in range(2):
+                        interaction_pass(c0, width, t, g, acc[:, t - t0, :])
+                if t0 == 0 or not shared:
                     for t in (t0, t0 + 1):
                         nc.scalar.activation(y[:, t, :], acc[:, t - t0, :], ACT.Identity, bias=bias[0][:, t : t + 1])
                 else:
@@ -218,37 +231,83 @@ def tile_list_mixture_geomean_interactions_kernel(
                     )
             nc.sync.dma_start(y_rows[:, :, c0 : c0 + width], y[:])
 
-        def out_planes(c0, width):
-            y_bf = ring.tile([P, 4 * width], BF16, name="y_bf", tag="y_bf", align_bytes=64)
+        y_bfs = {}
+
+        def round_y(c0, width):
+            y_bf = y_bfs[c0] = held([P, 4 * width], BF16, "y_bf%d" % c0)
             nc.vector.tensor_copy(
                 y_bf[:].rearrange("p (c i t) -> p c t i", i=4, t=4),
                 ys[c0][:].rearrange("p t (c i) -> p c t i", i=4),
             )
-            y_w = held([P, width], I32, "y_w%d" % c0)
-            nc.vector.quantize_mx(out=y_w[:].bitcast(FP8X4), scales=y_sc[:, c0 : c0 + width], in_=y_bf[:])
-            nc.sync.dma_start(y_words[:, c0 : c0 + width], y_w[:])
 
-        chunks = [(0,256),(256,256),(512,256),(768,256)]
+        def out_planes(c0, width):
+            y_bf = y_bfs[c0]
+            cols = slice(c0, c0 + width)
+            nc.vector.quantize_mx(out=y_w[:, cols].bitcast(FP8X4), scales=y_sc[:, cols], in_=y_bf[:])
+
+        def store_words(lo, hi):
+            nc.sync.dma_start(y_words[:, lo:hi], y_w[:, lo:hi])
+
+        c = [(0, 256), (256, 256), (512, 256), (768, 128), (896, 128)]
         energy(0, [0, 1])
+        round_ws(0, 0)
         quantise_ws(0, 0)
+        round_ws(1, 0)
         quantise_ws(1, 0)
         energy(1, [0])
+        round_ws(0, 1)
+        size(0, *c[0])
         quantise_ws(0, 1)
-        quantise_ws(1, 1)
-        size(0, *chunks[0])
-        deal_wi()
-        size(1, *chunks[0])
-        size(0, *chunks[1])
-        size(1, *chunks[1])
-        interactions(*chunks[0])
+        size(0, *c[1])
+        round_ws(1, 1)
+        root(0, *c[0])
+        root(0, *c[1])
         energy(1, [1])
-        for i in range(2, len(chunks)):
-            size(0, *chunks[i])
-            size(1, *chunks[i])
-            interactions(*chunks[i - 1])
-        interactions(*chunks[-1])
-        for c in chunks:
-            out_planes(*c)
+        size(0, *c[2])
+        quantise_ws(1, 1)
+        size(0, *c[3])
+        size(0, *c[4])
+        quantise_h(0, *c[0])
+        root(0, *c[2])
+        size(1, *c[0])
+        root(0, *c[3])
+        root(0, *c[4])
+        deal_wi()
+        root(1, *c[0])
+        size(1, *c[1])
+        quantise_h(1, *c[0])
+        quantise_h(0, *c[1])
+        root(1, *c[1])
+        interactions(*c[0])
+        size(1, *c[2])
+        quantise_h(1, *c[1])
+        quantise_h(0, *c[2])
+        root(1, *c[2])
+        interactions(*c[1])
+        size(1, *c[3])
+        size(1, *c[4])
+        quantise_h(0, *c[3])
+        quantise_h(0, *c[4])
+        quantise_h(1, *c[2])
+        root(1, *c[3])
+        root(1, *c[4])
+        interactions(*c[2])
+        round_y(*c[0])
+        quantise_h(1, *c[3])
+        quantise_h(1, *c[4])
+        interactions(*c[3])
+        interactions(*c[4])
+        out_planes(*c[0])
+        round_y(*c[1])
+        round_y(*c[2])
+        out_planes(*c[1])
+        store_words(0, 512)
+        out_planes(*c[2])
+        round_y(*c[3])
+        round_y(*c[4])
+        out_planes(*c[3])
+        out_planes(*c[4])
+        store_words(512, S)
         for q in range(4):
             eng = nc.scalar if q % 2 else nc.sync
             eng.dma_start(out_2[0, 4 * q : 4 * q + 4, :].bitcast(I32), y_sc[32 * q : 32 * q + 4, :].bitcast(I32))

@@ -51,7 +51,7 @@ def tile_list_mixture_geomean_interactions_kernel(
         nc.gpsimd.memset(planes[1][:].bitcast(I32), 0)
         nc.scalar.activation(warm_out[:], warm[:], ACT.Sqrt)
 
-        we_raw = held([P, 2, PASS], I32, "we_raw")
+        we_raw = keep.tile([P, 2, PASS], I32, name="we_raw", tag="we_raw", align_bytes=64)
         nc.sync.dma_start(we_raw[:], we_words.rearrange("a p c -> p a c").bitcast(I32))
         tab_w = []
         for a, tag in enumerate(("first", "second")):
@@ -89,25 +89,27 @@ def tile_list_mixture_geomean_interactions_kernel(
                 cols = slice(jh * HALF // 16, (jh + 1) * HALF // 16)
                 nc.vector.tensor_copy(v_w[a, jh][:], tab_w[a][:].bitcast(U32).indirect(offsets[:, cols]))
 
-        ws_all = keep.tile([P, 2, 2, 4, PASS], F32, name="ws_all", tag="first", align_bytes=64)
+        ws_all = keep.tile([P, 2, 2, 4, PASS], F32, name="ws_all", tag="we_raw", align_bytes=64)
         ws_raw = {}
         for g in range(2):
             for a in range(2):
                 ws_raw[a, g] = ws_all[:, g, a, :, :]
                 block = ws[PASS * a : PASS * (a + 1), PASS * g : PASS * (g + 1)]
                 nc.sync.dma_start(ws_raw[a, g], block.rearrange("(p j) c -> p j c", j=4))
-        wi_raw = keep.tile([P, 2, PASS], I32, name="wi_raw", tag="second", align_bytes=64)
+        wi_raw = keep.tile([P, 2, PASS], I32, name="wi_raw", tag="first", align_bytes=64)
         nc.sync.dma_start(wi_raw[:], wi_words.rearrange("a p c i -> p a (c i)").bitcast(I32))
 
         ws_w, ws_sc = {}, {}
 
         ws_bf = {}
+        ws_tag = {(0, 0): "second", (1, 0): "second", (0, 1): "second", (1, 1): "second"}
 
-        def round_ws(a, g):
-            ws_bf[a, g] = held([P, 4 * PASS], BF16, "ws_bf%d%d" % (a, g))
-            nc.vector.tensor_copy(
-                ws_bf[a, g][:].rearrange("p (t m j) -> p m j t", t=4, j=4),
-                ws_raw[a, g].rearrange("p j (m t) -> p m j t", t=4),
+        def round_ws(a, g, cast=nc.vector.tensor_copy, m=slice(0, P)):
+            if (a, g) not in ws_bf:
+                ws_bf[a, g] = keep.tile([P, 4 * PASS], BF16, name="ws_bf%d%d" % (a, g), tag=ws_tag[a, g], align_bytes=64)
+            cast(
+                ws_bf[a, g][:].rearrange("p (t m j) -> p m j t", t=4, j=4)[:, m],
+                ws_raw[a, g].rearrange("p j (m t) -> p m j t", t=4)[:, m],
             )
 
         def quantise_ws(a, g):
@@ -117,39 +119,49 @@ def tile_list_mixture_geomean_interactions_kernel(
 
         pos_energy = {}
 
-        def energy(g, halves):
-            accs = {}
-            banks = [(jh, t) for jh in halves for t in range(4)]
-            if g == 0:
-                steps = [(a, bank) for a in range(2) for bank in banks]
-            else:
-                steps = [(a, bank) for bank in banks for a in range(2)]
-            for jh in halves:
-                pos_energy[g, jh] = held([P, 4, HALF], F32, "pos_energy%d%d" % (g, jh))
-            for a, (jh, t) in steps:
-                if a == 0:
-                    accs[jh, t] = psum.tile([P, HALF], F32, name="acc", tag="acc")
-                c0 = PASS * g + P * t
-                nc.tensor.matmul_mx(
-                    out=accs[jh, t][:],
-                    lhsT=we_w[a][:, 2 * c0 : 2 * (c0 + P)].bitcast(FP4X4),
-                    lhsT_scale=we_sc[a][:, c0 : c0 + P],
-                    rhs=v_w[a, jh][:].bitcast(FP8X4),
-                    rhs_scale=v_sc[a][:, jh * HALF : (jh + 1) * HALF],
-                    start=(a == 0),
-                    stop=(a == 1),
-                )
-                if a == 1:
-                    nc.scalar.activation(pos_energy[g, jh][:, t, :], accs[jh, t][:], ACT.Relu)
+        energy_acc = {}
+        for g in range(2):
+            for jh in range(2):
+                pos_energy[g, jh] = keep.tile([P, 4, HALF], F32, name="pos_energy%d%d" % (g, jh), tag="energy%d%d" % (g, jh), align_bytes=64)
+
+        def energy_pass(g, jh, t, a):
+            if a == 0:
+                energy_acc[g, jh, t] = psum.tile([P, HALF], F32, name="acc", tag="acc")
+            c0 = PASS * g + P * t
+            nc.tensor.matmul_mx(
+                out=energy_acc[g, jh, t][:],
+                lhsT=we_w[a][:, 2 * c0 : 2 * (c0 + P)].bitcast(FP4X4),
+                lhsT_scale=we_sc[a][:, c0 : c0 + P],
+                rhs=v_w[a, jh][:].bitcast(FP8X4),
+                rhs_scale=v_sc[a][:, jh * HALF : (jh + 1) * HALF],
+                start=(a == 0),
+                stop=(a == 1),
+            )
+
+        def relu_scalar(g, jh, t):
+            nc.scalar.activation(pos_energy[g, jh][:, t, :], energy_acc[g, jh, t][:], ACT.Relu)
+
+        def relu_vector(g, jh, t):
+            nc.vector.tensor_scalar(
+                out=pos_energy[g, jh][:, t, :], in0=energy_acc[g, jh, t][:], scalar1=0.0, scalar2=None, op0=ALU.max
+            )
+
+        def energy(g, jh, on_scalar=range(4)):
+            for t in range(4):
+                for a in range(2):
+                    energy_pass(g, jh, t, a)
+                if t in on_scalar:
+                    relu_scalar(g, jh, t)
 
         h_w, h_sc, prods, h_bfs = {}, {}, {}, {}
 
+        size_acc = {}
+
         def size(g, c0, width):
             jh, lo = divmod(c0, HALF)
-            prod = prods[g, c0] = held([P, 4, width], F32, "prod%d_%d" % (g, c0))
             per = HALF // width
             for t0 in range(0, 4, per):
-                acc = psum.tile([P, per, width], F32, name="acc", tag="acc")
+                acc = size_acc[g, c0, t0] = psum.tile([P, per, width], F32, name="acc", tag="acc")
                 for t in range(t0, t0 + per):
                     for a in (1, 0):
                         nc.tensor.matmul_mx(
@@ -161,9 +173,15 @@ def tile_list_mixture_geomean_interactions_kernel(
                             start=(a == 1),
                             stop=(a == 0),
                         )
+
+        def product(g, c0, width):
+            jh, lo = divmod(c0, HALF)
+            per = HALF // width
+            prod = prods[g, c0] = held([P, 4, width], F32, "prod%d_%d" % (g, c0))
+            for t0 in range(0, 4, per):
                 nc.vector.scalar_tensor_tensor(
                     out=prod[:, t0 : t0 + per, :],
-                    in0=acc[:],
+                    in0=size_acc[g, c0, t0][:],
                     scalar=0.0,
                     in1=pos_energy[g, jh][:, t0 : t0 + per, lo : lo + width],
                     op0=ALU.max,
@@ -185,11 +203,13 @@ def tile_list_mixture_geomean_interactions_kernel(
             h_sc[g, c0] = held([P, width], U8, "h_sc%d_%d" % (g, c0))
             nc.vector.quantize_mx(out=h_w[g, c0][:].bitcast(FP8X4), scales=h_sc[g, c0][:], in_=h_bf[:])
 
-        wi_w = held([P, 2, N], I32, "wi_w")
+        dealt_wi = []
 
         bias = []
 
         def deal_wi():
+            wi_w = keep.tile([P, 2, N], I32, name="wi_w", tag="second", align_bytes=64)
+            dealt_wi.append(wi_w)
             bias.append(keep.tile([P, 4], F32, name="bias", tag="we_w0", align_bytes=64))
             nc.sync.dma_start(bias[0][:], b.rearrange("(p t) -> p t", t=4))
             nc.vector.tensor_copy(
@@ -204,15 +224,15 @@ def tile_list_mixture_geomean_interactions_kernel(
 
         ys = {}
 
-        def interaction_pass(c0, width, t, g, acc):
+        def interaction_pass(c0, width, t, g, acc, first=1):
             nc.tensor.matmul_mx(
                 out=acc,
-                lhsT=wi_w[:, g, P * t : P * (t + 1)].bitcast(FP8X4),
+                lhsT=dealt_wi[0][:, g, P * t : P * (t + 1)].bitcast(FP8X4),
                 lhsT_scale=wi_sc[g][:, P * t : P * (t + 1)],
                 rhs=h_w[g, c0][:].bitcast(FP8X4),
                 rhs_scale=h_sc[g, c0][:],
-                start=(g == 0),
-                stop=(g == 1),
+                start=(g == first),
+                stop=(g != first),
             )
 
         def interactions(c0, width, shared=False):
@@ -220,7 +240,7 @@ def tile_list_mixture_geomean_interactions_kernel(
             for t0 in (0, 2):
                 acc = psum.tile([P, 2, width], F32, name="acc", tag="acc")
                 for t in (t0, t0 + 1):
-                    for g in range(2):
+                    for g in (1, 0):
                         interaction_pass(c0, width, t, g, acc[:, t - t0, :])
                 if t0 == 0 or not shared:
                     for t in (t0, t0 + 1):
@@ -231,11 +251,30 @@ def tile_list_mixture_geomean_interactions_kernel(
                     )
             nc.sync.dma_start(y_rows[:, :, c0 : c0 + width], y[:])
 
+        last_acc = {}
+
+        def open_last(c0, width):
+            for t in range(4):
+                last_acc[t] = psum.tile([P, width], F32, name="acc", tag="acc")
+                interaction_pass(c0, width, t, 0, last_acc[t][:], 0)
+
+        def close_last(c0, width):
+            y = ys[c0] = held([P, 4, width], F32, "y%d" % c0)
+            for t in range(4):
+                interaction_pass(c0, width, t, 1, last_acc[t][:], 0)
+                if t % 2 == 0:
+                    nc.scalar.activation(y[:, t, :], last_acc[t][:], ACT.Identity, bias=bias[0][:, t : t + 1])
+                else:
+                    nc.vector.tensor_scalar(
+                        out=y[:, t, :], in0=last_acc[t][:], scalar1=bias[0][:, t : t + 1], scalar2=None, op0=ALU.add
+                    )
+            nc.sync.dma_start(y_rows[:, :, c0 : c0 + width], y[:])
+
         y_bfs = {}
 
-        def round_y(c0, width):
+        def round_y(c0, width, cast=nc.vector.tensor_copy):
             y_bf = y_bfs[c0] = held([P, 4 * width], BF16, "y_bf%d" % c0)
-            nc.vector.tensor_copy(
+            cast(
                 y_bf[:].rearrange("p (c i t) -> p c t i", i=4, t=4),
                 ys[c0][:].rearrange("p t (c i) -> p c t i", i=4),
             )
@@ -249,65 +288,82 @@ def tile_list_mixture_geomean_interactions_kernel(
             nc.sync.dma_start(y_words[:, lo:hi], y_w[:, lo:hi])
 
         c = [(0, 256), (256, 256), (512, 256), (768, 128), (896, 128)]
-        energy(0, [0, 1])
+        for a in range(2):
+            for t in range(4):
+                energy_pass(0, 0, t, a)
+                if a == 1:
+                    relu_scalar(0, 0, t)
+        energy(0, 1)
         round_ws(0, 0)
         quantise_ws(0, 0)
+        energy(1, 0)
         round_ws(1, 0)
         quantise_ws(1, 0)
-        energy(1, [0])
         round_ws(0, 1)
         size(0, *c[0])
-        quantise_ws(0, 1)
+        energy(1, 1)
         size(0, *c[1])
-        round_ws(1, 1)
-        root(0, *c[0])
-        root(0, *c[1])
-        energy(1, [1])
         size(0, *c[2])
+        product(0, *c[0])
+        root(0, *c[0])
+        quantise_ws(0, 1)
+        round_ws(1, 1)
+        product(0, *c[1])
+        root(0, *c[1])
         quantise_ws(1, 1)
-        size(0, *c[3])
-        size(0, *c[4])
-        quantise_h(0, *c[0])
-        root(0, *c[2])
         size(1, *c[0])
-        root(0, *c[3])
-        root(0, *c[4])
-        deal_wi()
-        root(1, *c[0])
         size(1, *c[1])
-        quantise_h(1, *c[0])
-        quantise_h(0, *c[1])
-        root(1, *c[1])
-        interactions(*c[0])
+        product(0, *c[2])
+        root(0, *c[2])
+        deal_wi()
+        quantise_h(0, *c[0])
+        product(1, *c[0])
+        root(1, *c[0])
         size(1, *c[2])
-        quantise_h(1, *c[1])
-        quantise_h(0, *c[2])
-        root(1, *c[2])
-        interactions(*c[1])
+        product(1, *c[1])
+        size(0, *c[3])
         size(1, *c[3])
+        quantise_h(1, *c[0])
+        interactions(*c[0])
+        root(1, *c[1])
+        quantise_h(0, *c[1])
+        product(1, *c[2])
+        size(0, *c[4])
         size(1, *c[4])
-        quantise_h(0, *c[3])
-        quantise_h(0, *c[4])
+        quantise_h(1, *c[1])
+        interactions(*c[1])
+        root(1, *c[2])
+        product(0, *c[3])
+        product(1, *c[3])
+        quantise_h(0, *c[2])
+        product(0, *c[4])
+        product(1, *c[4])
         quantise_h(1, *c[2])
+        root(0, *c[3])
         root(1, *c[3])
+        interactions(*c[2], True)
+        root(0, *c[4])
         root(1, *c[4])
-        interactions(*c[2])
-        round_y(*c[0])
+        quantise_h(0, *c[3])
         quantise_h(1, *c[3])
+        quantise_h(0, *c[4])
+        interactions(*c[3], False)
+        open_last(*c[4])
         quantise_h(1, *c[4])
-        interactions(*c[3])
-        interactions(*c[4])
-        out_planes(*c[0])
+        close_last(*c[4])
+        round_y(*c[0])
         round_y(*c[1])
-        round_y(*c[2])
+        out_planes(*c[0])
         out_planes(*c[1])
         store_words(0, 512)
-        out_planes(*c[2])
+        round_y(*c[2])
         round_y(*c[3])
-        round_y(*c[4])
+        out_planes(*c[2])
         out_planes(*c[3])
+        store_words(512, 896)
+        round_y(*c[4])
         out_planes(*c[4])
-        store_words(512, S)
+        store_words(896, S)
         for q in range(4):
             eng = nc.scalar if q % 2 else nc.sync
             eng.dma_start(out_2[0, 4 * q : 4 * q + 4, :].bitcast(I32), y_sc[32 * q : 32 * q + 4, :].bitcast(I32))

@@ -124,8 +124,8 @@ def tile_list_mixture_geomean_interactions_kernel(
             for jh in range(2):
                 pos_energy[g, jh] = keep.tile([P, 4, HALF], F32, name="pos_energy%d%d" % (g, jh), tag="energy%d%d" % (g, jh), align_bytes=64)
 
-        def energy_pass(g, jh, t, a):
-            if a == 0:
+        def energy_pass(g, jh, t, a, first=0):
+            if a == first:
                 energy_acc[g, jh, t] = psum.tile([P, HALF], F32, name="acc", tag="acc")
             c0 = PASS * g + P * t
             nc.tensor.matmul_mx(
@@ -134,8 +134,8 @@ def tile_list_mixture_geomean_interactions_kernel(
                 lhsT_scale=we_sc[a][:, c0 : c0 + P],
                 rhs=v_w[a, jh][:].bitcast(FP8X4),
                 rhs_scale=v_sc[a][:, jh * HALF : (jh + 1) * HALF],
-                start=(a == 0),
-                stop=(a == 1),
+                start=(a == first),
+                stop=(a != first),
             )
 
         def relu_scalar(g, jh, t):
@@ -148,8 +148,8 @@ def tile_list_mixture_geomean_interactions_kernel(
 
         def energy(g, jh, on_scalar=range(4)):
             for t in range(4):
-                for a in range(2):
-                    energy_pass(g, jh, t, a)
+                for a in (1, 0):
+                    energy_pass(g, jh, t, a, 1)
                 if t in on_scalar:
                     relu_scalar(g, jh, t)
 
@@ -225,12 +225,13 @@ def tile_list_mixture_geomean_interactions_kernel(
         ys = {}
 
         def interaction_pass(c0, width, t, g, acc, first=1):
+            start = c0 if (g, c0) in h_w else 768
             nc.tensor.matmul_mx(
                 out=acc,
                 lhsT=dealt_wi[0][:, g, P * t : P * (t + 1)].bitcast(FP8X4),
                 lhsT_scale=wi_sc[g][:, P * t : P * (t + 1)],
-                rhs=h_w[g, c0][:].bitcast(FP8X4),
-                rhs_scale=h_sc[g, c0][:],
+                rhs=h_w[g, start][:, c0 - start : c0 - start + width].bitcast(FP8X4),
+                rhs_scale=h_sc[g, start][:, c0 - start : c0 - start + width],
                 start=(g == first),
                 stop=(g != first),
             )
@@ -287,7 +288,10 @@ def tile_list_mixture_geomean_interactions_kernel(
         def store_words(lo, hi):
             nc.sync.dma_start(y_words[:, lo:hi], y_w[:, lo:hi])
 
-        c = [(0, 256), (256, 256), (512, 256), (768, 128), (896, 128)]
+        wide = [(0, 256), (256, 256), (512, 256)]
+        narrow = [(768, 128), (896, 128)]
+        chunks = wide + narrow
+        units = [(g, chunk) for g in range(2) for chunk in wide] + [(g, chunk) for chunk in narrow for g in range(2)]
         for a in range(2):
             for t in range(4):
                 energy_pass(0, 0, t, a)
@@ -300,70 +304,46 @@ def tile_list_mixture_geomean_interactions_kernel(
         round_ws(1, 0)
         quantise_ws(1, 0)
         round_ws(0, 1)
-        size(0, *c[0])
+        size(0, *wide[0])
         energy(1, 1)
-        size(0, *c[1])
-        size(0, *c[2])
-        product(0, *c[0])
-        root(0, *c[0])
+        size(0, *wide[1])
+        size(0, *wide[2])
+        product(0, *wide[0])
+        root(0, *wide[0])
         quantise_ws(0, 1)
         round_ws(1, 1)
-        product(0, *c[1])
-        root(0, *c[1])
+        product(0, *wide[1])
+        root(0, *wide[1])
         quantise_ws(1, 1)
-        size(1, *c[0])
-        size(1, *c[1])
-        product(0, *c[2])
-        root(0, *c[2])
-        deal_wi()
-        quantise_h(0, *c[0])
-        product(1, *c[0])
-        root(1, *c[0])
-        size(1, *c[2])
-        product(1, *c[1])
-        size(0, *c[3])
-        size(1, *c[3])
-        quantise_h(1, *c[0])
-        interactions(*c[0])
-        root(1, *c[1])
-        quantise_h(0, *c[1])
-        product(1, *c[2])
-        size(0, *c[4])
-        size(1, *c[4])
-        quantise_h(1, *c[1])
-        interactions(*c[1])
-        root(1, *c[2])
-        product(0, *c[3])
-        product(1, *c[3])
-        quantise_h(0, *c[2])
-        product(0, *c[4])
-        product(1, *c[4])
-        quantise_h(1, *c[2])
-        root(0, *c[3])
-        root(1, *c[3])
-        interactions(*c[2], True)
-        root(0, *c[4])
-        root(1, *c[4])
-        quantise_h(0, *c[3])
-        quantise_h(1, *c[3])
-        quantise_h(0, *c[4])
-        interactions(*c[3], False)
-        open_last(*c[4])
-        quantise_h(1, *c[4])
-        close_last(*c[4])
-        round_y(*c[0])
-        round_y(*c[1])
-        out_planes(*c[0])
-        out_planes(*c[1])
-        store_words(0, 512)
-        round_y(*c[2])
-        round_y(*c[3])
-        out_planes(*c[2])
-        out_planes(*c[3])
-        store_words(512, 896)
-        round_y(*c[4])
-        out_planes(*c[4])
-        store_words(896, S)
+        for g, chunk in units[3 : 2 + 3]:
+            size(g, *chunk)
+        for i in range(2, len(units) + 1):
+            if i + 3 < len(units):
+                size(units[i + 3][0], *units[i + 3][1])
+            if i < len(units):
+                product(units[i][0], *units[i][1])
+            if i == 2:
+                deal_wi()
+            g, chunk = units[i - 1]
+            if g == 1:
+                quantise_h(0, *chunk)
+                if chunk == chunks[-1]:
+                    open_last(*chunk)
+                    quantise_h(1, *chunk)
+                    close_last(*chunk)
+                else:
+                    quantise_h(1, *chunk)
+                    interactions(*chunk, chunk in wide[2:])
+            if i < len(units):
+                root(units[i][0], *units[i][1])
+        round_y(*chunks[0])
+        for before, chunk in zip(chunks, chunks[1:] + [None]):
+            if chunk:
+                round_y(*chunk)
+            out_planes(*before)
+            end = before[0] + before[1]
+            if end in {512: 0, 768: 512, S: 768}:
+                store_words({512: 0, 768: 512, S: 768}[end], end)
         for q in range(4):
             eng = nc.scalar if q % 2 else nc.sync
             eng.dma_start(out_2[0, 4 * q : 4 * q + 4, :].bitcast(I32), y_sc[32 * q : 32 * q + 4, :].bitcast(I32))

@@ -45,9 +45,9 @@ def tile_list_mixture_geomean_interactions_kernel(
         nc.sync.dma_start(w_sc_raw[0:32, 0:H].bitcast(I32), we_scales.rearrange("a q c -> (a q) c").bitcast(I32))
         nc.sync.dma_start(w_sc_raw[0:32, H:].bitcast(I32), wi_scales.rearrange("a q c -> (a q) c").bitcast(I32))
         nc.vector.memset(warm[:], 1.0)
-        for lo, hi in ((32, 64), (64, P)):
-            nc.vector.memset(tab_sc[lo:hi, :].bitcast(I32), 0)
-            nc.gpsimd.memset(w_sc_raw[lo:hi, :].bitcast(I32), 0)
+        for raw in (tab_sc, w_sc_raw):
+            for lo, hi in ((32, 64), (64, P)):
+                nc.vector.memset(raw[lo:hi, :].bitcast(I32), 0)
         nc.gpsimd.memset(planes[1][:].bitcast(I32), 0)
         nc.scalar.activation(warm_out[:], warm[:], ACT.Sqrt)
 
@@ -61,8 +61,12 @@ def tile_list_mixture_geomean_interactions_kernel(
         picked_sc = keep.tile([P, S], U8, name="picked_sc", tag="we_w0", align_bytes=64)
         nc.vector.tensor_copy(picked_sc[:], tab_sc[:].indirect(offsets[:]))
         nc.vector.tensor_copy(
-            rows[:, S:].rearrange("p (g t m) -> p g t m", g=3, t=4),
-            w_sc_raw[:].rearrange("p (g m t) -> p g t m", g=3, t=4),
+            rows[:, S : S + H].rearrange("p (g t m) -> p g t m", g=2, t=4),
+            w_sc_raw[:, 0:H].rearrange("p (g m t) -> p g t m", g=2, t=4),
+        )
+        nc.vector.tensor_copy(
+            rows[:, S + H :].rearrange("p (t m) -> p t m", t=4),
+            w_sc_raw[:, H:].rearrange("p (m t) -> p t m", t=4),
         )
         nc.vector.tensor_copy(rows[:, 0:S].bitcast(I32), picked_sc[:].bitcast(I32))
 
@@ -293,11 +297,11 @@ def tile_list_mixture_geomean_interactions_kernel(
         chunks = wide + narrow
         units = [(g, chunk) for g in range(2) for chunk in wide] + [(g, chunk) for chunk in narrow for g in range(2)]
         for a in range(2):
-            for t in range(4):
-                energy_pass(0, 0, t, a)
-                if a == 1:
-                    relu_scalar(0, 0, t)
-        energy(0, 1)
+            for jh in range(2):
+                for t in range(4):
+                    energy_pass(0, jh, t, a)
+                    if a == 1:
+                        relu_scalar(0, jh, t)
         round_ws(0, 0)
         quantise_ws(0, 0)
         energy(1, 0)
@@ -305,8 +309,8 @@ def tile_list_mixture_geomean_interactions_kernel(
         quantise_ws(1, 0)
         round_ws(0, 1)
         size(0, *wide[0])
-        energy(1, 1)
         size(0, *wide[1])
+        energy(1, 1)
         size(0, *wide[2])
         product(0, *wide[0])
         root(0, *wide[0])

@@ -56,7 +56,9 @@ def tile_list_mixture_geomean_interactions_kernel(
         tab_w = []
         for a, tag in enumerate(("first", "second")):
             tab_w.append(keep.tile([P, T], I32, name="tab_w%d" % a, tag=tag, align_bytes=64))
-            nc.sync.dma_start(tab_w[a][:], tab_words[a].rearrange("p t i -> p (t i)").bitcast(I32))
+            words = tab_words[a].rearrange("p t i -> p (t i)").bitcast(I32)
+            for lo, hi in ((0, T),) if a == 0 else ((0, T // 4), (T // 4, T)):
+                nc.sync.dma_start(tab_w[a][:, lo:hi], words[:, lo:hi])
 
         picked_sc = keep.tile([P, S], U8, name="picked_sc", tag="we_w0", align_bytes=64)
         nc.vector.tensor_copy(picked_sc[:], tab_sc[:].indirect(offsets[:]))
@@ -106,7 +108,7 @@ def tile_list_mixture_geomean_interactions_kernel(
         ws_w, ws_sc = {}, {}
 
         ws_bf = {}
-        ws_tag = {(0, 0): "second", (1, 0): "second", (0, 1): "second", (1, 1): "second"}
+        ws_tag = {(0, 0): "second", (1, 0): "other", (0, 1): "second", (1, 1): "other"}
 
         def round_ws(a, g, cast=nc.vector.tensor_copy, m=slice(0, P)):
             if (a, g) not in ws_bf:
@@ -212,7 +214,7 @@ def tile_list_mixture_geomean_interactions_kernel(
         bias = []
 
         def deal_wi():
-            wi_w = keep.tile([P, 2, N], I32, name="wi_w", tag="second", align_bytes=64)
+            wi_w = keep.tile([P, 2, N], I32, name="wi_w", tag="other", align_bytes=64)
             dealt_wi.append(wi_w)
             bias.append(keep.tile([P, 4], F32, name="bias", tag="we_w0", align_bytes=64))
             nc.sync.dma_start(bias[0][:], b.rearrange("(p t) -> p t", t=4))

@@ -92,8 +92,10 @@ def tile_list_mixture_geomean_interactions_kernel(
         for a in range(2):
             for jh in range(2):
                 v_w[a, jh] = held([P, HALF], U32, "v_w%d%d" % (a, jh))
-                cols = slice(jh * HALF // 16, (jh + 1) * HALF // 16)
-                nc.vector.tensor_copy(v_w[a, jh][:], tab_w[a][:].bitcast(U32).indirect(offsets[:, cols]))
+                step = HALF // 2 if (a, jh) == (1, 0) else HALF
+                for lo in range(0, HALF, step):
+                    cols = slice((jh * HALF + lo) // 16, (jh * HALF + lo + step) // 16)
+                    nc.vector.tensor_copy(v_w[a, jh][:, lo : lo + step], tab_w[a][:].bitcast(U32).indirect(offsets[:, cols]))
 
         ws_all = keep.tile([P, 2, 2, 4, PASS], F32, name="ws_all", tag="we_raw", align_bytes=64)
         ws_raw = {}
@@ -144,6 +146,22 @@ def tile_list_mixture_geomean_interactions_kernel(
                 stop=(a != first),
             )
 
+        def first_passes(lo, t0, a):
+            if a == 0:
+                energy_acc[lo, t0] = psum.tile([P, 2, HALF // 2], F32, name="acc", tag="acc")
+            for t in (t0, t0 + 1):
+                nc.tensor.matmul_mx(
+                    out=energy_acc[lo, t0][:, t - t0, :],
+                    lhsT=we_w[a][:, 2 * P * t : 2 * P * (t + 1)].bitcast(FP4X4),
+                    lhsT_scale=we_sc[a][:, P * t : P * (t + 1)],
+                    rhs=v_w[a, 0][:, lo : lo + HALF // 2].bitcast(FP8X4),
+                    rhs_scale=v_sc[a][:, lo : lo + HALF // 2],
+                    start=(a == 0 and t == t0),
+                    stop=(a == 1 and t == t0 + 1),
+                )
+            if a == 1:
+                nc.scalar.activation(pos_energy[0, 0][:, t0 : t0 + 2, lo : lo + HALF // 2], energy_acc[lo, t0][:], ACT.Relu)
+
         def relu_scalar(g, jh, t):
             nc.scalar.activation(pos_energy[g, jh][:, t, :], energy_acc[g, jh, t][:], ACT.Relu)
 
@@ -152,12 +170,11 @@ def tile_list_mixture_geomean_interactions_kernel(
                 out=pos_energy[g, jh][:, t, :], in0=energy_acc[g, jh, t][:], scalar1=0.0, scalar2=None, op0=ALU.max
             )
 
-        def energy(g, jh, on_scalar=range(4)):
-            for t in range(4):
+        def energy(g, jh, slices=range(4)):
+            for t in slices:
                 for a in (1, 0):
                     energy_pass(g, jh, t, a, 1)
-                if t in on_scalar:
-                    relu_scalar(g, jh, t)
+                relu_scalar(g, jh, t)
 
         h_w, h_sc, prods, h_bfs = {}, {}, {}, {}
 
@@ -218,9 +235,9 @@ def tile_list_mixture_geomean_interactions_kernel(
             dealt_wi.append(wi_w)
             bias.append(keep.tile([P, 4], F32, name="bias", tag="we_w0", align_bytes=64))
             nc.sync.dma_start(bias[0][:], b.rearrange("(p t) -> p t", t=4))
-            nc.vector.tensor_copy(
-                wi_w[:].rearrange("p a (t o i) -> p a o t i", t=4, i=4),
-                wi_raw[:].rearrange("p a (o i t) -> p a o t i", t=4, i=4),
+            nc.scalar.copy(
+                wi_w[:].bitcast(U32).rearrange("p a (t o i) -> p a o t i", t=4, i=4),
+                wi_raw[:].bitcast(U32).rearrange("p a (o i t) -> p a o t i", t=4, i=4),
             )
 
         y_sc = held([P, S], U8, "y_sc")
@@ -299,20 +316,23 @@ def tile_list_mixture_geomean_interactions_kernel(
         chunks = wide + narrow
         units = [(g, chunk) for g in range(2) for chunk in wide] + [(g, chunk) for chunk in narrow for g in range(2)]
         for a in range(2):
-            for jh in range(2):
-                for t in range(4):
-                    energy_pass(0, jh, t, a)
-                    if a == 1:
-                        relu_scalar(0, jh, t)
+            for lo in (0, HALF // 2):
+                for t0 in (0, 2):
+                    first_passes(lo, t0, a)
+            for t in range(4):
+                energy_pass(0, 1, t, a)
+                if a == 1:
+                    relu_scalar(0, 1, t)
         round_ws(0, 0)
         quantise_ws(0, 0)
         energy(1, 0)
+        energy(1, 1, (0, 1))
         round_ws(1, 0)
         quantise_ws(1, 0)
         round_ws(0, 1)
         size(0, *wide[0])
         size(0, *wide[1])
-        energy(1, 1)
+        energy(1, 1, (2, 3))
         size(0, *wide[2])
         product(0, *wide[0])
         root(0, *wide[0])

@@ -18,7 +18,18 @@ ALU = mybir.AluOpType
 
 P = 128
 PASS = 512
-HALF = 512
+BANK = 512
+PER_COLUMN = 16
+SCALE_ROWS = 32
+
+WIDE = [(0, 256), (256, 256), (512, 256)]
+NARROW = [(768, 128), (896, 128)]
+CHUNKS = WIDE + NARROW
+STEPS = [(g, chunk) for g in range(2) for chunk in WIDE] + [(g, chunk) for chunk in NARROW for g in range(2)]
+AHEAD = 3
+SHARED_CHUNK = WIDE[2]
+TABLE_LOADS = [[(0, T)], [(0, T // 4), (T // 4, T)]]
+WORD_STORES = {256: 0, 768: 256, S: 768}
 
 
 def tile_list_mixture_geomean_interactions_kernel(
@@ -29,95 +40,95 @@ def tile_list_mixture_geomean_interactions_kernel(
         keep = ctx.enter_context(tc.tile_pool(name="keep", bufs=1))
         psum = ctx.enter_context(tc.psum_pool(name="psum", bufs=8))
 
-        def held(shape, dtype, name):
-            return keep.tile(shape, dtype, name=name, align_bytes=64)
+        def held(shape, dtype, name, tag=None):
+            return keep.tile(shape, dtype, name=name, tag=tag or name, align_bytes=64)
 
-        offsets = keep.tile([P, S // 16], U16, name="offsets")
+        def bank(shape):
+            return psum.tile(shape, F32, name="acc", tag="acc")
+
+        offsets = keep.tile([P, S // PER_COLUMN], U16, name="offsets")
         nc.sync.dma_start(offsets[:], offs)
 
         tab_sc = held([P, T], U8, "tab_sc")
         w_sc_raw = held([P, H + N], U8, "w_sc_raw")
         planes = [held([P, S + H + N], U8, "planes%d" % a) for a in range(2)]
-        rows = planes[0]
         warm = held([P, 16], F32, "warm")
         warm_out = held([P, 16], F32, "warm_out")
-        nc.sync.dma_start(tab_sc[0:32, :].bitcast(I32), tab_scales.rearrange("a q t -> (a q) t").bitcast(I32))
-        nc.sync.dma_start(w_sc_raw[0:32, 0:H].bitcast(I32), we_scales.rearrange("a q c -> (a q) c").bitcast(I32))
-        nc.sync.dma_start(w_sc_raw[0:32, H:].bitcast(I32), wi_scales.rearrange("a q c -> (a q) c").bitcast(I32))
+        flat = slice(0, SCALE_ROWS)
+        nc.sync.dma_start(tab_sc[flat, :].bitcast(I32), tab_scales.rearrange("a q t -> (a q) t").bitcast(I32))
+        nc.sync.dma_start(w_sc_raw[flat, 0:H].bitcast(I32), we_scales.rearrange("a q c -> (a q) c").bitcast(I32))
+        nc.sync.dma_start(w_sc_raw[flat, H:].bitcast(I32), wi_scales.rearrange("a q c -> (a q) c").bitcast(I32))
         nc.vector.memset(warm[:], 1.0)
         for raw in (tab_sc, w_sc_raw):
-            for lo, hi in ((32, 64), (64, P)):
+            for lo, hi in ((SCALE_ROWS, 64), (64, P)):
                 nc.vector.memset(raw[lo:hi, :].bitcast(I32), 0)
         nc.gpsimd.memset(planes[1][:].bitcast(I32), 0)
         nc.scalar.activation(warm_out[:], warm[:], ACT.Sqrt)
 
-        we_raw = keep.tile([P, 2, PASS], I32, name="we_raw", tag="we_raw", align_bytes=64)
+        we_raw = held([P, 2, PASS], I32, "we_raw")
         nc.sync.dma_start(we_raw[:], we_words.rearrange("a p c -> p a c").bitcast(I32))
         tab_w = []
-        for a, tag in enumerate(("first", "second")):
-            tab_w.append(keep.tile([P, T], I32, name="tab_w%d" % a, tag=tag, align_bytes=64))
+        for a in range(2):
+            tab_w.append(held([P, T], I32, "tab_w%d" % a))
             words = tab_words[a].rearrange("p t i -> p (t i)").bitcast(I32)
-            for lo, hi in ((0, T),) if a == 0 else ((0, T // 4), (T // 4, T)):
+            for lo, hi in TABLE_LOADS[a]:
                 nc.sync.dma_start(tab_w[a][:, lo:hi], words[:, lo:hi])
 
-        picked_sc = keep.tile([P, S], U8, name="picked_sc", tag="we_w0", align_bytes=64)
+        picked_sc = held([P, S], U8, "picked_sc")
         nc.vector.tensor_copy(picked_sc[:], tab_sc[:].indirect(offsets[:]))
         nc.vector.tensor_copy(
-            rows[:, S : S + H].rearrange("p (g t m) -> p g t m", g=2, t=4),
+            planes[0][:, S : S + H].rearrange("p (g t m) -> p g t m", g=2, t=4),
             w_sc_raw[:, 0:H].rearrange("p (g m t) -> p g t m", g=2, t=4),
         )
         nc.vector.tensor_copy(
-            rows[:, S + H :].rearrange("p (t m) -> p t m", t=4),
+            planes[0][:, S + H :].rearrange("p (t m) -> p t m", t=4),
             w_sc_raw[:, H:].rearrange("p (m t) -> p t m", t=4),
         )
-        nc.vector.tensor_copy(rows[:, 0:S].bitcast(I32), picked_sc[:].bitcast(I32))
+        nc.vector.tensor_copy(planes[0][:, 0:S].bitcast(I32), picked_sc[:].bitcast(I32))
 
-        for a in range(2):
-            for q in range(4):
-                r0 = 16 * a + 4 * q
-                if r0 > 0:
-                    eng = nc.gpsimd if (a, q) == (1, 3) else nc.scalar
-                    eng.dma_start(planes[a][32 * q : 32 * q + 4, :].bitcast(I32), rows[r0 : r0 + 4, :].bitcast(I32))
+        moves = [(a, q) for a in range(2) for q in range(4)][1:]
+        for a, q in moves:
+            queue = nc.gpsimd if (a, q) == moves[-1] else nc.scalar
+            row = 16 * a + 4 * q
+            queue.dma_start(planes[a][32 * q : 32 * q + 4, :].bitcast(I32), planes[0][row : row + 4, :].bitcast(I32))
         v_sc = [planes[a][:, 0:S] for a in range(2)]
         we_sc = [planes[a][:, S : S + H] for a in range(2)]
         wi_sc = [planes[a][:, S + H :] for a in range(2)]
 
-        we_all = keep.tile([P, 2, 2 * H], U8, name="we_all", tag="we_w0", align_bytes=64)
+        we_dealt = held([P, 2, 2 * H], U8, "we_dealt", "picked_sc")
         nc.vector.tensor_copy(
-            we_all[:].bitcast(U16).rearrange("p a (g t m) -> p (a g) t m", g=2, t=4),
+            we_dealt[:].bitcast(U16).rearrange("p a (g t m) -> p (a g) t m", g=2, t=4),
             we_raw[:].bitcast(U16).rearrange("p a (g m t) -> p (a g) t m", g=2, t=4),
         )
-        we_w = [we_all[:, a, :] for a in range(2)]
+
         v_w = {}
         for a in range(2):
-            for jh in range(2):
-                v_w[a, jh] = held([P, HALF], U32, "v_w%d%d" % (a, jh))
-                step = HALF // 2 if (a, jh) == (1, 0) else HALF
-                for lo in range(0, HALF, step):
-                    cols = slice((jh * HALF + lo) // 16, (jh * HALF + lo + step) // 16)
-                    nc.vector.tensor_copy(v_w[a, jh][:, lo : lo + step], tab_w[a][:].bitcast(U32).indirect(offsets[:, cols]))
+            for half in range(2):
+                v_w[a, half] = held([P, BANK], U32, "v_w%d%d" % (a, half))
+                entries = BANK // 2 if (a, half) == (1, 0) else BANK
+                for lo in range(0, BANK, entries):
+                    first = half * BANK + lo
+                    part = offsets[:, first // PER_COLUMN : (first + entries) // PER_COLUMN]
+                    nc.vector.tensor_copy(v_w[a, half][:, lo : lo + entries], tab_w[a][:].bitcast(U32).indirect(part))
 
-        ws_all = keep.tile([P, 2, 2, 4, PASS], F32, name="ws_all", tag="we_raw", align_bytes=64)
+        ws_all = held([P, 2, 2, 4, PASS], F32, "ws_all", "we_raw")
         ws_raw = {}
         for g in range(2):
             for a in range(2):
                 ws_raw[a, g] = ws_all[:, g, a, :, :]
                 block = ws[PASS * a : PASS * (a + 1), PASS * g : PASS * (g + 1)]
                 nc.sync.dma_start(ws_raw[a, g], block.rearrange("(p j) c -> p j c", j=4))
-        wi_raw = keep.tile([P, 2, PASS], I32, name="wi_raw", tag="first", align_bytes=64)
+        wi_raw = held([P, 2, PASS], I32, "wi_raw", "tab_w0")
         nc.sync.dma_start(wi_raw[:], wi_words.rearrange("a p c i -> p a (c i)").bitcast(I32))
 
-        ws_w, ws_sc = {}, {}
+        ws_bf, ws_w, ws_sc = {}, {}, {}
+        round_tags = ["tab_w1", "rounded"]
 
-        ws_bf = {}
-        ws_tag = {(0, 0): "second", (1, 0): "other", (0, 1): "second", (1, 1): "other"}
-
-        def round_ws(a, g, cast=nc.vector.tensor_copy, m=slice(0, P)):
-            if (a, g) not in ws_bf:
-                ws_bf[a, g] = keep.tile([P, 4 * PASS], BF16, name="ws_bf%d%d" % (a, g), tag=ws_tag[a, g], align_bytes=64)
-            cast(
-                ws_bf[a, g][:].rearrange("p (t m j) -> p m j t", t=4, j=4)[:, m],
-                ws_raw[a, g].rearrange("p j (m t) -> p m j t", t=4)[:, m],
+        def round_ws(a, g):
+            ws_bf[a, g] = held([P, 4 * PASS], BF16, "ws_bf%d%d" % (a, g), round_tags[a])
+            nc.vector.tensor_copy(
+                ws_bf[a, g][:].rearrange("p (t m u e) -> p m u t e", t=4, u=2, e=2),
+                ws_raw[a, g].rearrange("p (u e) (m t) -> p m u t e", t=4, e=2),
             )
 
         def quantise_ws(a, g):
@@ -125,251 +136,238 @@ def tile_list_mixture_geomean_interactions_kernel(
             ws_sc[a, g] = held([P, PASS], U8, "ws_sc%d%d" % (a, g))
             nc.vector.quantize_mx(out=ws_w[a, g][:].bitcast(FP8X4), scales=ws_sc[a, g][:], in_=ws_bf[a, g][:])
 
-        pos_energy = {}
-
-        energy_acc = {}
+        pos_energy, energy_acc = {}, {}
         for g in range(2):
-            for jh in range(2):
-                pos_energy[g, jh] = keep.tile([P, 4, HALF], F32, name="pos_energy%d%d" % (g, jh), tag="energy%d%d" % (g, jh), align_bytes=64)
+            for half in range(2):
+                pos_energy[g, half] = held([P, 4, BANK], F32, "pos_energy%d%d" % (g, half))
 
-        def energy_pass(g, jh, t, a, first=0):
-            if a == first:
-                energy_acc[g, jh, t] = psum.tile([P, HALF], F32, name="acc", tag="acc")
-            c0 = PASS * g + P * t
+        def energy_matmul(out, g, t, a, c0, width, start, stop):
+            half, lo = divmod(c0, BANK)
+            col = PASS * g + P * t
             nc.tensor.matmul_mx(
-                out=energy_acc[g, jh, t][:],
-                lhsT=we_w[a][:, 2 * c0 : 2 * (c0 + P)].bitcast(FP4X4),
-                lhsT_scale=we_sc[a][:, c0 : c0 + P],
-                rhs=v_w[a, jh][:].bitcast(FP8X4),
-                rhs_scale=v_sc[a][:, jh * HALF : (jh + 1) * HALF],
-                start=(a == first),
-                stop=(a != first),
+                out=out,
+                lhsT=we_dealt[:, a, 2 * col : 2 * (col + P)].bitcast(FP4X4),
+                lhsT_scale=we_sc[a][:, col : col + P],
+                rhs=v_w[a, half][:, lo : lo + width].bitcast(FP8X4),
+                rhs_scale=v_sc[a][:, c0 : c0 + width],
+                start=start,
+                stop=stop,
             )
 
-        def first_passes(lo, t0, a):
+        def energy_pair(c0, width, t0, a):
             if a == 0:
-                energy_acc[lo, t0] = psum.tile([P, 2, HALF // 2], F32, name="acc", tag="acc")
+                energy_acc[c0, t0] = bank([P, 2, width])
+            acc = energy_acc[c0, t0]
             for t in (t0, t0 + 1):
-                nc.tensor.matmul_mx(
-                    out=energy_acc[lo, t0][:, t - t0, :],
-                    lhsT=we_w[a][:, 2 * P * t : 2 * P * (t + 1)].bitcast(FP4X4),
-                    lhsT_scale=we_sc[a][:, P * t : P * (t + 1)],
-                    rhs=v_w[a, 0][:, lo : lo + HALF // 2].bitcast(FP8X4),
-                    rhs_scale=v_sc[a][:, lo : lo + HALF // 2],
-                    start=(a == 0 and t == t0),
-                    stop=(a == 1 and t == t0 + 1),
-                )
+                energy_matmul(acc[:, t - t0, :], 0, t, a, c0, width, a == 0 and t == t0, a == 1 and t == t0 + 1)
             if a == 1:
-                nc.scalar.activation(pos_energy[0, 0][:, t0 : t0 + 2, lo : lo + HALF // 2], energy_acc[lo, t0][:], ACT.Relu)
+                nc.scalar.activation(pos_energy[0, 0][:, t0 : t0 + 2, c0 : c0 + width], acc[:], ACT.Relu)
 
-        def relu_scalar(g, jh, t):
-            nc.scalar.activation(pos_energy[g, jh][:, t, :], energy_acc[g, jh, t][:], ACT.Relu)
+        def energy_pass(g, half, t, a, opening):
+            if a == opening:
+                energy_acc[g, half, t] = bank([P, BANK])
+            acc = energy_acc[g, half, t]
+            energy_matmul(acc[:], g, t, a, half * BANK, BANK, a == opening, a != opening)
+            if a != opening:
+                nc.scalar.activation(pos_energy[g, half][:, t, :], acc[:], ACT.Relu)
 
-        def relu_vector(g, jh, t):
-            nc.vector.tensor_scalar(
-                out=pos_energy[g, jh][:, t, :], in0=energy_acc[g, jh, t][:], scalar1=0.0, scalar2=None, op0=ALU.max
-            )
-
-        def energy(g, jh, slices=range(4)):
+        def energy_banks(g, half, slices):
             for t in slices:
                 for a in (1, 0):
-                    energy_pass(g, jh, t, a, 1)
-                relu_scalar(g, jh, t)
+                    energy_pass(g, half, t, a, 1)
 
-        h_w, h_sc, prods, h_bfs = {}, {}, {}, {}
+        size_acc, prod, h_bf, h_w, h_sc = {}, {}, {}, {}, {}
 
-        size_acc = {}
-
-        def size(g, c0, width):
-            jh, lo = divmod(c0, HALF)
-            per = HALF // width
-            for t0 in range(0, 4, per):
-                acc = size_acc[g, c0, t0] = psum.tile([P, per, width], F32, name="acc", tag="acc")
-                for t in range(t0, t0 + per):
+        def size(g, chunk):
+            c0, width = chunk
+            half, lo = divmod(c0, BANK)
+            per_bank = BANK // width
+            for t0 in range(0, 4, per_bank):
+                acc = size_acc[g, c0, t0] = bank([P, per_bank, width])
+                for t in range(t0, t0 + per_bank):
                     for a in (1, 0):
                         nc.tensor.matmul_mx(
                             out=acc[:, t - t0, :],
                             lhsT=ws_w[a, g][:, P * t : P * (t + 1)].bitcast(FP8X4),
                             lhsT_scale=ws_sc[a, g][:, P * t : P * (t + 1)],
-                            rhs=v_w[a, jh][:, lo : lo + width].bitcast(FP8X4),
+                            rhs=v_w[a, half][:, lo : lo + width].bitcast(FP8X4),
                             rhs_scale=v_sc[a][:, c0 : c0 + width],
                             start=(a == 1),
                             stop=(a == 0),
                         )
 
-        def product(g, c0, width):
-            jh, lo = divmod(c0, HALF)
-            per = HALF // width
-            prod = prods[g, c0] = held([P, 4, width], F32, "prod%d_%d" % (g, c0))
-            for t0 in range(0, 4, per):
+        def product(g, chunk):
+            c0, width = chunk
+            half, lo = divmod(c0, BANK)
+            per_bank = BANK // width
+            prod[g, c0] = held([P, 4, width], F32, "prod%d_%d" % (g, c0))
+            for t0 in range(0, 4, per_bank):
                 nc.vector.scalar_tensor_tensor(
-                    out=prod[:, t0 : t0 + per, :],
+                    out=prod[g, c0][:, t0 : t0 + per_bank, :],
                     in0=size_acc[g, c0, t0][:],
                     scalar=0.0,
-                    in1=pos_energy[g, jh][:, t0 : t0 + per, lo : lo + width],
+                    in1=pos_energy[g, half][:, t0 : t0 + per_bank, lo : lo + width],
                     op0=ALU.max,
                     op1=ALU.mult,
                 )
 
-        def root(g, c0, width):
-            prod = prods[g, c0]
-            h_bf = h_bfs[g, c0] = held([P, 4 * width], BF16, "h_bf%d_%d" % (g, c0))
-            nc.scalar.activation(
-                h_bf[:].rearrange("p (c i t) -> p c t i", i=4, t=4),
-                prod[:].rearrange("p t (c i) -> p c t i", i=4),
-                ACT.Sqrt,
-            )
+        def words_of(tile):
+            return tile[:].rearrange("p (c i t) -> p c t i", i=4, t=4)
 
-        def quantise_h(g, c0, width):
-            h_bf = h_bfs[g, c0]
+        def slices_of(tile):
+            return tile[:].rearrange("p t (c i) -> p c t i", i=4)
+
+        def root(g, chunk):
+            c0, width = chunk
+            h_bf[g, c0] = held([P, 4 * width], BF16, "h_bf%d_%d" % (g, c0))
+            nc.scalar.activation(words_of(h_bf[g, c0]), slices_of(prod[g, c0]), ACT.Sqrt)
+
+        def quantise_h(g, chunk):
+            c0, width = chunk
             h_w[g, c0] = held([P, width], U32, "h_w%d_%d" % (g, c0))
             h_sc[g, c0] = held([P, width], U8, "h_sc%d_%d" % (g, c0))
-            nc.vector.quantize_mx(out=h_w[g, c0][:].bitcast(FP8X4), scales=h_sc[g, c0][:], in_=h_bf[:])
+            nc.vector.quantize_mx(out=h_w[g, c0][:].bitcast(FP8X4), scales=h_sc[g, c0][:], in_=h_bf[g, c0][:])
 
-        dealt_wi = []
-
-        bias = []
+        late = {}
 
         def deal_wi():
-            wi_w = keep.tile([P, 2, N], I32, name="wi_w", tag="other", align_bytes=64)
-            dealt_wi.append(wi_w)
-            bias.append(keep.tile([P, 4], F32, name="bias", tag="we_w0", align_bytes=64))
-            nc.sync.dma_start(bias[0][:], b.rearrange("(p t) -> p t", t=4))
+            late["wi_w"] = held([P, 2, N], I32, "wi_w", round_tags[1])
+            late["bias"] = held([P, 4], F32, "bias", "picked_sc")
+            nc.sync.dma_start(late["bias"][:], b.rearrange("(p t) -> p t", t=4))
             nc.scalar.copy(
-                wi_w[:].bitcast(U32).rearrange("p a (t o i) -> p a o t i", t=4, i=4),
-                wi_raw[:].bitcast(U32).rearrange("p a (o i t) -> p a o t i", t=4, i=4),
+                late["wi_w"][:].bitcast(U32).rearrange("p a (t m) -> p a m t", t=4),
+                wi_raw[:].bitcast(U32).rearrange("p a (m t) -> p a m t", t=4),
             )
 
         y_sc = held([P, S], U8, "y_sc")
         y_w = held([P, S], I32, "y_w")
         y_rows = out_0.rearrange("(p t) j -> p t j", t=4)
         y_words = out_1[0].rearrange("p m i -> p (m i)").bitcast(I32)
+        y, y_bf, last_acc = {}, {}, {}
 
-        ys = {}
-
-        def interaction_pass(c0, width, t, g, acc, first=1):
-            start = c0 if (g, c0) in h_w else 768
+        def interaction_pass(out, c0, t, g, opening):
             nc.tensor.matmul_mx(
-                out=acc,
-                lhsT=dealt_wi[0][:, g, P * t : P * (t + 1)].bitcast(FP8X4),
+                out=out,
+                lhsT=late["wi_w"][:, g, P * t : P * (t + 1)].bitcast(FP8X4),
                 lhsT_scale=wi_sc[g][:, P * t : P * (t + 1)],
-                rhs=h_w[g, start][:, c0 - start : c0 - start + width].bitcast(FP8X4),
-                rhs_scale=h_sc[g, start][:, c0 - start : c0 - start + width],
-                start=(g == first),
-                stop=(g != first),
+                rhs=h_w[g, c0][:].bitcast(FP8X4),
+                rhs_scale=h_sc[g, c0][:],
+                start=(g == opening),
+                stop=(g != opening),
             )
 
-        def interactions(c0, width, shared=False):
-            y = ys[c0] = held([P, 4, width], F32, "y%d" % c0)
+        def add_bias(c0, t, acc):
+            nc.scalar.activation(y[c0][:, t, :], acc, ACT.Identity, bias=late["bias"][:, t : t + 1])
+
+        def interactions(chunk):
+            c0, width = chunk
+            y[c0] = held([P, 4, width], F32, "y%d" % c0)
             for t0 in (0, 2):
-                acc = psum.tile([P, 2, width], F32, name="acc", tag="acc")
+                acc = bank([P, 2, width])
                 for t in (t0, t0 + 1):
                     for g in (1, 0):
-                        interaction_pass(c0, width, t, g, acc[:, t - t0, :])
-                if t0 == 0 or not shared:
-                    for t in (t0, t0 + 1):
-                        nc.scalar.activation(y[:, t, :], acc[:, t - t0, :], ACT.Identity, bias=bias[0][:, t : t + 1])
+                        interaction_pass(acc[:, t - t0, :], c0, t, g, 1)
+                if t0 == 2 and chunk == SHARED_CHUNK:
+                    spread = late["bias"][:, 2:4].unsqueeze(2).to_broadcast([P, 2, width])
+                    nc.vector.tensor_tensor(y[c0][:, 2:4, :], acc[:], spread, ALU.add)
                 else:
-                    nc.vector.tensor_tensor(
-                        y[:, 2:4, :], acc[:], bias[0][:, 2:4].unsqueeze(2).to_broadcast([P, 2, width]), ALU.add
-                    )
-            nc.sync.dma_start(y_rows[:, :, c0 : c0 + width], y[:])
+                    for t in (t0, t0 + 1):
+                        add_bias(c0, t, acc[:, t - t0, :])
+            nc.sync.dma_start(y_rows[:, :, c0 : c0 + width], y[c0][:])
 
-        last_acc = {}
-
-        def open_last(c0, width):
+        def open_last(chunk):
+            c0, width = chunk
             for t in range(4):
-                last_acc[t] = psum.tile([P, width], F32, name="acc", tag="acc")
-                interaction_pass(c0, width, t, 0, last_acc[t][:], 0)
+                last_acc[t] = bank([P, width])
+                interaction_pass(last_acc[t][:], c0, t, 0, 0)
 
-        def close_last(c0, width):
-            y = ys[c0] = held([P, 4, width], F32, "y%d" % c0)
+        def close_last(chunk):
+            c0, width = chunk
+            y[c0] = held([P, 4, width], F32, "y%d" % c0)
             for t in range(4):
-                interaction_pass(c0, width, t, 1, last_acc[t][:], 0)
+                interaction_pass(last_acc[t][:], c0, t, 1, 0)
                 if t % 2 == 0:
-                    nc.scalar.activation(y[:, t, :], last_acc[t][:], ACT.Identity, bias=bias[0][:, t : t + 1])
+                    add_bias(c0, t, last_acc[t][:])
                 else:
                     nc.vector.tensor_scalar(
-                        out=y[:, t, :], in0=last_acc[t][:], scalar1=bias[0][:, t : t + 1], scalar2=None, op0=ALU.add
+                        out=y[c0][:, t, :],
+                        in0=last_acc[t][:],
+                        scalar1=late["bias"][:, t : t + 1],
+                        scalar2=None,
+                        op0=ALU.add,
                     )
-            nc.sync.dma_start(y_rows[:, :, c0 : c0 + width], y[:])
+            nc.sync.dma_start(y_rows[:, :, c0 : c0 + width], y[c0][:])
 
-        y_bfs = {}
+        def round_y(chunk):
+            c0, width = chunk
+            y_bf[c0] = held([P, 4 * width], BF16, "y_bf%d" % c0)
+            nc.vector.tensor_copy(words_of(y_bf[c0]), slices_of(y[c0]))
 
-        def round_y(c0, width, cast=nc.vector.tensor_copy):
-            y_bf = y_bfs[c0] = held([P, 4 * width], BF16, "y_bf%d" % c0)
-            cast(
-                y_bf[:].rearrange("p (c i t) -> p c t i", i=4, t=4),
-                ys[c0][:].rearrange("p t (c i) -> p c t i", i=4),
-            )
+        def quantise_y(chunk):
+            c0, width = chunk
+            end = c0 + width
+            nc.vector.quantize_mx(out=y_w[:, c0:end].bitcast(FP8X4), scales=y_sc[:, c0:end], in_=y_bf[c0][:])
+            if end in WORD_STORES:
+                nc.sync.dma_start(y_words[:, WORD_STORES[end] : end], y_w[:, WORD_STORES[end] : end])
 
-        def out_planes(c0, width):
-            y_bf = y_bfs[c0]
-            cols = slice(c0, c0 + width)
-            nc.vector.quantize_mx(out=y_w[:, cols].bitcast(FP8X4), scales=y_sc[:, cols], in_=y_bf[:])
-
-        def store_words(lo, hi):
-            nc.sync.dma_start(y_words[:, lo:hi], y_w[:, lo:hi])
-
-        wide = [(0, 256), (256, 256), (512, 256)]
-        narrow = [(768, 128), (896, 128)]
-        chunks = wide + narrow
-        units = [(g, chunk) for g in range(2) for chunk in wide] + [(g, chunk) for chunk in narrow for g in range(2)]
         for a in range(2):
-            for lo in (0, HALF // 2):
+            for c0, width in WIDE[:2]:
                 for t0 in (0, 2):
-                    first_passes(lo, t0, a)
+                    energy_pair(c0, width, t0, a)
             for t in range(4):
-                energy_pass(0, 1, t, a)
-                if a == 1:
-                    relu_scalar(0, 1, t)
+                energy_pass(0, 1, t, a, 0)
+
         round_ws(0, 0)
         quantise_ws(0, 0)
-        energy(1, 0)
-        energy(1, 1, (0, 1))
+        energy_banks(1, 0, range(4))
+        energy_banks(1, 1, range(1))
         round_ws(1, 0)
         quantise_ws(1, 0)
         round_ws(0, 1)
-        size(0, *wide[0])
-        size(0, *wide[1])
-        energy(1, 1, (2, 3))
-        size(0, *wide[2])
-        product(0, *wide[0])
-        root(0, *wide[0])
+        size(*STEPS[0])
+        size(*STEPS[1])
+        energy_banks(1, 1, range(1, 4))
+        size(*STEPS[2])
+        product(*STEPS[0])
+        root(*STEPS[0])
         quantise_ws(0, 1)
         round_ws(1, 1)
-        product(0, *wide[1])
-        root(0, *wide[1])
+        product(*STEPS[1])
+        root(*STEPS[1])
         quantise_ws(1, 1)
-        for g, chunk in units[3 : 2 + 3]:
-            size(g, *chunk)
-        for i in range(2, len(units) + 1):
-            if i + 3 < len(units):
-                size(units[i + 3][0], *units[i + 3][1])
-            if i < len(units):
-                product(units[i][0], *units[i][1])
-            if i == 2:
+
+        begun = 2
+        for step in STEPS[begun + 1 : begun + AHEAD]:
+            size(*step)
+        for i in range(begun, len(STEPS) + 1):
+            if i + AHEAD < len(STEPS):
+                size(*STEPS[i + AHEAD])
+            if i < len(STEPS):
+                product(*STEPS[i])
+            if i == begun:
                 deal_wi()
-            g, chunk = units[i - 1]
+            g, chunk = STEPS[i - 1]
             if g == 1:
-                quantise_h(0, *chunk)
-                if chunk == chunks[-1]:
-                    open_last(*chunk)
-                    quantise_h(1, *chunk)
-                    close_last(*chunk)
+                if chunk == CHUNKS[1]:
+                    round_y(CHUNKS[0])
+                quantise_h(0, chunk)
+                if chunk == CHUNKS[1]:
+                    quantise_y(CHUNKS[0])
+                if chunk == CHUNKS[-1]:
+                    open_last(chunk)
+                    quantise_h(1, chunk)
+                    close_last(chunk)
                 else:
-                    quantise_h(1, *chunk)
-                    interactions(*chunk, chunk in wide[2:])
-            if i < len(units):
-                root(units[i][0], *units[i][1])
-        round_y(*chunks[0])
-        for before, chunk in zip(chunks, chunks[1:] + [None]):
-            if chunk:
-                round_y(*chunk)
-            out_planes(*before)
-            end = before[0] + before[1]
-            if end in {512: 0, 768: 512, S: 768}:
-                store_words({512: 0, 768: 512, S: 768}[end], end)
+                    quantise_h(1, chunk)
+                    interactions(chunk)
+            if i < len(STEPS):
+                root(*STEPS[i])
+
+        round_y(CHUNKS[1])
+        for chunk, following in zip(CHUNKS[1:], CHUNKS[2:] + [None]):
+            if following:
+                round_y(following)
+            quantise_y(chunk)
         for q in range(4):
-            eng = nc.scalar if q % 2 else nc.sync
-            eng.dma_start(out_2[0, 4 * q : 4 * q + 4, :].bitcast(I32), y_sc[32 * q : 32 * q + 4, :].bitcast(I32))
+            queue = nc.scalar if q % 2 else nc.sync
+            queue.dma_start(out_2[0, 4 * q : 4 * q + 4, :].bitcast(I32), y_sc[32 * q : 32 * q + 4, :].bitcast(I32))

@@ -19,6 +19,7 @@ ALU = mybir.AluOpType
 P = 128
 PASS = 512
 BANK = 512
+QUARTER = 256
 PER_COLUMN = 16
 SCALE_ROWS = 32
 
@@ -138,89 +139,87 @@ def tile_list_mixture_geomean_interactions_kernel(
 
         pos_energy, energy_acc = {}, {}
         for g in range(2):
-            for half in range(2):
-                pos_energy[g, half] = held([P, 4, BANK], F32, "pos_energy%d%d" % (g, half))
+            for c0, width in CHUNKS:
+                pos_energy[g, c0] = held([P, 2, width, 2], F32, "pos_energy%d_%d" % (g, c0))
+
+        def gathered(a, c0, width):
+            half, lo = divmod(c0, BANK)
+            return v_w[a, half][:, lo : lo + width].bitcast(FP8X4), v_sc[a][:, c0 : c0 + width]
 
         def energy_matmul(out, g, t, a, c0, width, start, stop):
-            half, lo = divmod(c0, BANK)
             col = PASS * g + P * t
+            words, scales = gathered(a, c0, width)
             nc.tensor.matmul_mx(
                 out=out,
                 lhsT=we_dealt[:, a, 2 * col : 2 * (col + P)].bitcast(FP4X4),
                 lhsT_scale=we_sc[a][:, col : col + P],
-                rhs=v_w[a, half][:, lo : lo + width].bitcast(FP8X4),
-                rhs_scale=v_sc[a][:, c0 : c0 + width],
+                rhs=words,
+                rhs_scale=scales,
                 start=start,
                 stop=stop,
             )
 
-        def energy_pair(c0, width, t0, a):
-            if a == 0:
-                energy_acc[c0, t0] = bank([P, 2, width])
-            acc = energy_acc[c0, t0]
-            for t in (t0, t0 + 1):
-                energy_matmul(acc[:, t - t0, :], 0, t, a, c0, width, a == 0 and t == t0, a == 1 and t == t0 + 1)
-            if a == 1:
-                nc.scalar.activation(pos_energy[0, 0][:, t0 : t0 + 2, c0 : c0 + width], acc[:], ACT.Relu)
-
-        def energy_pass(g, half, t, a, opening):
+        def energy_pass(g, c0, u, a, opening):
             if a == opening:
-                energy_acc[g, half, t] = bank([P, BANK])
-            acc = energy_acc[g, half, t]
-            energy_matmul(acc[:], g, t, a, half * BANK, BANK, a == opening, a != opening)
+                energy_acc[g, c0, u] = bank([P, 2, QUARTER])
+            acc = energy_acc[g, c0, u]
+            for e in range(2):
+                energy_matmul(acc[:, e, :], g, 2 * u + e, a, c0, QUARTER, a == opening and e == 0, a != opening and e == 1)
             if a != opening:
-                nc.scalar.activation(pos_energy[g, half][:, t, :], acc[:], ACT.Relu)
+                for lo, width in CHUNKS:
+                    if c0 <= lo < c0 + QUARTER:
+                        part = acc[:, :, lo - c0 : lo - c0 + width].rearrange("p e c -> p c e")
+                        nc.scalar.activation(pos_energy[g, lo][:, u, :, :], part, ACT.Relu)
 
-        def energy_banks(g, half, slices):
-            for t in slices:
+        def energy_banks(g, banks):
+            for c0, u in banks:
                 for a in (1, 0):
-                    energy_pass(g, half, t, a, 1)
+                    energy_pass(g, c0, u, a, 1)
 
         size_acc, prod, h_bf, h_w, h_sc = {}, {}, {}, {}, {}
 
         def size(g, chunk):
             c0, width = chunk
-            half, lo = divmod(c0, BANK)
-            per_bank = BANK // width
-            for t0 in range(0, 4, per_bank):
-                acc = size_acc[g, c0, t0] = bank([P, per_bank, width])
-                for t in range(t0, t0 + per_bank):
-                    for a in (1, 0):
-                        nc.tensor.matmul_mx(
-                            out=acc[:, t - t0, :],
-                            lhsT=ws_w[a, g][:, P * t : P * (t + 1)].bitcast(FP8X4),
-                            lhsT_scale=ws_sc[a, g][:, P * t : P * (t + 1)],
-                            rhs=v_w[a, half][:, lo : lo + width].bitcast(FP8X4),
-                            rhs_scale=v_sc[a][:, c0 : c0 + width],
-                            start=(a == 1),
-                            stop=(a == 0),
-                        )
+            pairs = BANK // (2 * width)
+            for u0 in range(0, 2, pairs):
+                acc = size_acc[g, c0, u0] = bank([P, 2, pairs, width])
+                for u in range(u0, u0 + pairs):
+                    for e in range(2):
+                        t = 2 * u + e
+                        for a in (1, 0):
+                            words, scales = gathered(a, c0, width)
+                            nc.tensor.matmul_mx(
+                                out=acc[:, e, u - u0, :],
+                                lhsT=ws_w[a, g][:, P * t : P * (t + 1)].bitcast(FP8X4),
+                                lhsT_scale=ws_sc[a, g][:, P * t : P * (t + 1)],
+                                rhs=words,
+                                rhs_scale=scales,
+                                start=(a == 1),
+                                stop=(a == 0),
+                            )
 
         def product(g, chunk):
             c0, width = chunk
-            half, lo = divmod(c0, BANK)
-            per_bank = BANK // width
-            prod[g, c0] = held([P, 4, width], F32, "prod%d_%d" % (g, c0))
-            for t0 in range(0, 4, per_bank):
+            pairs = BANK // (2 * width)
+            prod[g, c0] = held([P, 2, width, 2], F32, "prod%d_%d" % (g, c0))
+            for u0 in range(0, 2, pairs):
                 nc.vector.scalar_tensor_tensor(
-                    out=prod[g, c0][:, t0 : t0 + per_bank, :],
-                    in0=size_acc[g, c0, t0][:],
+                    out=prod[g, c0][:, u0 : u0 + pairs, :, :].rearrange("p u c e -> p (u c) e"),
+                    in0=size_acc[g, c0, u0][:].rearrange("p e u c -> p (u c) e"),
                     scalar=0.0,
-                    in1=pos_energy[g, half][:, t0 : t0 + per_bank, lo : lo + width],
+                    in1=pos_energy[g, c0][:, u0 : u0 + pairs, :, :].rearrange("p u c e -> p (u c) e"),
                     op0=ALU.max,
                     op1=ALU.mult,
                 )
 
-        def words_of(tile):
-            return tile[:].rearrange("p (c i t) -> p c t i", i=4, t=4)
-
-        def slices_of(tile):
-            return tile[:].rearrange("p t (c i) -> p c t i", i=4)
-
         def root(g, chunk):
             c0, width = chunk
             h_bf[g, c0] = held([P, 4 * width], BF16, "h_bf%d_%d" % (g, c0))
-            nc.scalar.activation(words_of(h_bf[g, c0]), slices_of(prod[g, c0]), ACT.Sqrt)
+            nc.scalar.activation(
+                h_bf[g, c0][:].rearrange("p (c u e) -> p c u e", u=2, e=2),
+                prod[g, c0][:].rearrange("p u c e -> p c u e"),
+                ACT.Sqrt,
+            )
 
         def quantise_h(g, chunk):
             c0, width = chunk
@@ -301,7 +300,10 @@ def tile_list_mixture_geomean_interactions_kernel(
         def round_y(chunk):
             c0, width = chunk
             y_bf[c0] = held([P, 4 * width], BF16, "y_bf%d" % c0)
-            nc.vector.tensor_copy(words_of(y_bf[c0]), slices_of(y[c0]))
+            nc.vector.tensor_copy(
+                y_bf[c0][:].rearrange("p (c i t) -> p c t i", i=2, t=4),
+                y[c0][:].rearrange("p t (c i) -> p c t i", i=2),
+            )
 
         def quantise_y(chunk):
             c0, width = chunk
@@ -310,23 +312,20 @@ def tile_list_mixture_geomean_interactions_kernel(
             if end in WORD_STORES:
                 nc.sync.dma_start(y_words[:, WORD_STORES[end] : end], y_w[:, WORD_STORES[end] : end])
 
+        banks = [(c0, u) for c0 in range(0, S, QUARTER) for u in range(2)]
         for a in range(2):
-            for c0, width in WIDE[:2]:
-                for t0 in (0, 2):
-                    energy_pair(c0, width, t0, a)
-            for t in range(4):
-                energy_pass(0, 1, t, a, 0)
+            for c0, u in banks:
+                energy_pass(0, c0, u, a, 0)
 
         round_ws(0, 0)
         quantise_ws(0, 0)
-        energy_banks(1, 0, range(4))
-        energy_banks(1, 1, range(1))
+        energy_banks(1, banks[:5])
         round_ws(1, 0)
         quantise_ws(1, 0)
         round_ws(0, 1)
         size(*STEPS[0])
         size(*STEPS[1])
-        energy_banks(1, 1, range(1, 4))
+        energy_banks(1, banks[5:])
         size(*STEPS[2])
         product(*STEPS[0])
         root(*STEPS[0])

@@ -29,7 +29,7 @@ CHUNKS = WIDE + NARROW
 STEPS = [(g, chunk) for g in range(2) for chunk in WIDE] + [(g, chunk) for chunk in NARROW for g in range(2)]
 AHEAD = 3
 SHARED_CHUNK = WIDE[2]
-TABLE_LOADS = [[(0, T)], [(0, T // 4), (T // 4, T)]]
+TABLE_LOADS = [[(0, T)], [(0, T // 2), (T // 2, T)]]
 WORD_STORES = {256: 0, 768: 256, S: 768}
 
 
@@ -56,8 +56,8 @@ def tile_list_mixture_geomean_interactions_kernel(
         warm = held([P, 16], F32, "warm")
         warm_out = held([P, 16], F32, "warm_out")
         flat = slice(0, SCALE_ROWS)
-        nc.sync.dma_start(tab_sc[flat, :].bitcast(I32), tab_scales.rearrange("a q t -> (a q) t").bitcast(I32))
-        nc.sync.dma_start(w_sc_raw[flat, 0:H].bitcast(I32), we_scales.rearrange("a q c -> (a q) c").bitcast(I32))
+        nc.scalar.dma_start(tab_sc[flat, :].bitcast(I32), tab_scales.rearrange("a q t -> (a q) t").bitcast(I32))
+        nc.scalar.dma_start(w_sc_raw[flat, 0:H].bitcast(I32), we_scales.rearrange("a q c -> (a q) c").bitcast(I32))
         nc.sync.dma_start(w_sc_raw[flat, H:].bitcast(I32), wi_scales.rearrange("a q c -> (a q) c").bitcast(I32))
         nc.vector.memset(warm[:], 1.0)
         for raw in (tab_sc, w_sc_raw):

from contextlib import ExitStack

import concourse.mybir as mybir

K, T, S, H, N = 1024, 4096, 1024, 1024, 512
FLOPS = 2 * K * H * S * 2 + 2 * H * N * S

F32 = mybir.dt.float32
BF16 = mybir.dt.bfloat16
I32 = mybir.dt.int32
U32 = mybir.dt.uint32
U16 = mybir.dt.uint16
U8 = mybir.dt.uint8
FP8X4 = mybir.dt.float8_e4m3fn_x4
FP4X4 = mybir.dt.float4_e2m1fn_x4
ACT = mybir.ActivationFunctionType
ALU = mybir.AluOpType

P = 128
PASS = 512
BANK = 512
QUARTER = 256
PER_COLUMN = 16
SCALE_ROWS = 32

WIDE = [(0, 256), (256, 256), (512, 256)]
NARROW = [(768, 128), (896, 128)]
CHUNKS = WIDE + NARROW
STEPS = [(g, chunk) for g in range(2) for chunk in WIDE] + [(g, chunk) for chunk in NARROW for g in range(2)]
AHEAD = 3
SHARED_CHUNK = WIDE[2]
TABLE_LOADS = [[(0, T)], [(0, T // 2), (T // 2, T)]]
WORD_STORES = {256: 0, 768: 256, S: 768}


def tile_list_mixture_geomean_interactions_kernel(
    tc, tab_words, tab_scales, offs, ws, we_words, we_scales, wi_words, wi_scales, b, out_0, out_1, out_2
):
    nc = tc.nc
    with ExitStack() as ctx:
        keep = ctx.enter_context(tc.tile_pool(name="keep", bufs=1))
        psum = ctx.enter_context(tc.psum_pool(name="psum", bufs=8))

        def held(shape, dtype, name, tag=None):
            return keep.tile(shape, dtype, name=name, tag=tag or name, align_bytes=64)

        def bank(shape):
            return psum.tile(shape, F32, name="acc", tag="acc")

        offsets = keep.tile([P, S // PER_COLUMN], U16, name="offsets")
        nc.sync.dma_start(offsets[:], offs)

        tab_sc = held([P, T], U8, "tab_sc")
        w_sc_raw = held([P, H + N], U8, "w_sc_raw")
        planes = [held([P, S + H + N], U8, "planes%d" % a) for a in range(2)]
        warm = held([P, 16], F32, "warm")
        warm_out = held([P, 16], F32, "warm_out")
        flat = slice(0, SCALE_ROWS)
        nc.scalar.dma_start(tab_sc[flat, :].bitcast(I32), tab_scales.rearrange("a q t -> (a q) t").bitcast(I32))
        nc.scalar.dma_start(w_sc_raw[flat, 0:H].bitcast(I32), we_scales.rearrange("a q c -> (a q) c").bitcast(I32))
        nc.sync.dma_start(w_sc_raw[flat, H:].bitcast(I32), wi_scales.rearrange("a q c -> (a q) c").bitcast(I32))
        nc.vector.memset(warm[:], 1.0)
        for raw in (tab_sc, w_sc_raw):
            for lo, hi in ((SCALE_ROWS, 64), (64, P)):
                nc.vector.memset(raw[lo:hi, :].bitcast(I32), 0)
        nc.gpsimd.memset(planes[1][:].bitcast(I32), 0)
        nc.scalar.activation(warm_out[:], warm[:], ACT.Sqrt)

        we_raw = held([P, 2, PASS], I32, "we_raw")
        nc.sync.dma_start(we_raw[:], we_words.rearrange("a p c -> p a c").bitcast(I32))
        tab_w = []
        for a in range(2):
            tab_w.append(held([P, T], I32, "tab_w%d" % a))
            words = tab_words[a].rearrange("p t i -> p (t i)").bitcast(I32)
            for lo, hi in TABLE_LOADS[a]:
                nc.sync.dma_start(tab_w[a][:, lo:hi], words[:, lo:hi])

        picked_sc = held([P, S], U8, "picked_sc")
        nc.vector.tensor_copy(picked_sc[:], tab_sc[:].indirect(offsets[:]))
        nc.vector.tensor_copy(
            planes[0][:, S : S + H].rearrange("p (g t m) -> p g t m", g=2, t=4),
            w_sc_raw[:, 0:H].rearrange("p (g m t) -> p g t m", g=2, t=4),
        )
        nc.vector.tensor_copy(
            planes[0][:, S + H :].rearrange("p (t m) -> p t m", t=4),
            w_sc_raw[:, H:].rearrange("p (m t) -> p t m", t=4),
        )
        nc.vector.tensor_copy(planes[0][:, 0:S].bitcast(I32), picked_sc[:].bitcast(I32))

        moves = [(a, q) for a in range(2) for q in range(4)][1:]
        for a, q in moves:
            queue = nc.gpsimd if (a, q) == moves[-1] else nc.scalar
            row = 16 * a + 4 * q
            queue.dma_start(planes[a][32 * q : 32 * q + 4, :].bitcast(I32), planes[0][row : row + 4, :].bitcast(I32))
        v_sc = [planes[a][:, 0:S] for a in range(2)]
        we_sc = [planes[a][:, S : S + H] for a in range(2)]
        wi_sc = [planes[a][:, S + H :] for a in range(2)]

        we_dealt = held([P, 2, 2 * H], U8, "we_dealt", "picked_sc")
        nc.vector.tensor_copy(
            we_dealt[:].bitcast(U16).rearrange("p a (g t m) -> p (a g) t m", g=2, t=4),
            we_raw[:].bitcast(U16).rearrange("p a (g m t) -> p (a g) t m", g=2, t=4),
        )

        v_w = {}
        for a in range(2):
            for half in range(2):
                v_w[a, half] = held([P, BANK], U32, "v_w%d%d" % (a, half))
                entries = BANK // 2 if (a, half) == (1, 0) else BANK
                for lo in range(0, BANK, entries):
                    first = half * BANK + lo
                    part = offsets[:, first // PER_COLUMN : (first + entries) // PER_COLUMN]
                    nc.vector.tensor_copy(v_w[a, half][:, lo : lo + entries], tab_w[a][:].bitcast(U32).indirect(part))

        ws_all = held([P, 2, 2, 4, PASS], F32, "ws_all", "we_raw")
        ws_raw = {}
        for g in range(2):
            for a in range(2):
                ws_raw[a, g] = ws_all[:, g, a, :, :]
                block = ws[PASS * a : PASS * (a + 1), PASS * g : PASS * (g + 1)]
                nc.sync.dma_start(ws_raw[a, g], block.rearrange("(p j) c -> p j c", j=4))
        wi_raw = held([P, 2, PASS], I32, "wi_raw", "tab_w0")
        nc.sync.dma_start(wi_raw[:], wi_words.rearrange("a p c i -> p a (c i)").bitcast(I32))

        ws_bf, ws_w, ws_sc = {}, {}, {}
        round_tags = ["tab_w1", "rounded"]

        def round_ws(a, g):
            ws_bf[a, g] = held([P, 4 * PASS], BF16, "ws_bf%d%d" % (a, g), round_tags[a])
            nc.vector.tensor_copy(
                ws_bf[a, g][:].rearrange("p (t m u e) -> p m u t e", t=4, u=2, e=2),
                ws_raw[a, g].rearrange("p (u e) (m t) -> p m u t e", t=4, e=2),
            )

        def quantise_ws(a, g):
            ws_w[a, g] = held([P, PASS], U32, "ws_w%d%d" % (a, g))
            ws_sc[a, g] = held([P, PASS], U8, "ws_sc%d%d" % (a, g))
            nc.vector.quantize_mx(out=ws_w[a, g][:].bitcast(FP8X4), scales=ws_sc[a, g][:], in_=ws_bf[a, g][:])

        pos_energy, energy_acc = {}, {}
        for g in range(2):
            for c0, width in CHUNKS:
                pos_energy[g, c0] = held([P, 2, width, 2], F32, "pos_energy%d_%d" % (g, c0))

        def gathered(a, c0, width):
            half, lo = divmod(c0, BANK)
            return v_w[a, half][:, lo : lo + width].bitcast(FP8X4), v_sc[a][:, c0 : c0 + width]

        def energy_matmul(out, g, t, a, c0, width, start, stop):
            col = PASS * g + P * t
            words, scales = gathered(a, c0, width)
            nc.tensor.matmul_mx(
                out=out,
                lhsT=we_dealt[:, a, 2 * col : 2 * (col + P)].bitcast(FP4X4),
                lhsT_scale=we_sc[a][:, col : col + P],
                rhs=words,
                rhs_scale=scales,
                start=start,
                stop=stop,
            )

        def energy_pass(g, c0, u, a, opening):
            if a == opening:
                energy_acc[g, c0, u] = bank([P, 2, QUARTER])
            acc = energy_acc[g, c0, u]
            for e in range(2):
                energy_matmul(acc[:, e, :], g, 2 * u + e, a, c0, QUARTER, a == opening and e == 0, a != opening and e == 1)
            if a != opening:
                for lo, width in CHUNKS:
                    if c0 <= lo < c0 + QUARTER:
                        part = acc[:, :, lo - c0 : lo - c0 + width].rearrange("p e c -> p c e")
                        nc.scalar.activation(pos_energy[g, lo][:, u, :, :], part, ACT.Relu)

        def energy_banks(g, banks):
            for c0, u in banks:
                for a in (1, 0):
                    energy_pass(g, c0, u, a, 1)

        size_acc, prod, h_bf, h_w, h_sc = {}, {}, {}, {}, {}

        def size(g, chunk):
            c0, width = chunk
            pairs = BANK // (2 * width)
            for u0 in range(0, 2, pairs):
                acc = size_acc[g, c0, u0] = bank([P, 2, pairs, width])
                for u in range(u0, u0 + pairs):
                    for e in range(2):
                        t = 2 * u + e
                        for a in (1, 0):
                            words, scales = gathered(a, c0, width)
                            nc.tensor.matmul_mx(
                                out=acc[:, e, u - u0, :],
                                lhsT=ws_w[a, g][:, P * t : P * (t + 1)].bitcast(FP8X4),
                                lhsT_scale=ws_sc[a, g][:, P * t : P * (t + 1)],
                                rhs=words,
                                rhs_scale=scales,
                                start=(a == 1),
                                stop=(a == 0),
                            )

        def product(g, chunk):
            c0, width = chunk
            pairs = BANK // (2 * width)
            prod[g, c0] = held([P, 2, width, 2], F32, "prod%d_%d" % (g, c0))
            for u0 in range(0, 2, pairs):
                nc.vector.scalar_tensor_tensor(
                    out=prod[g, c0][:, u0 : u0 + pairs, :, :].rearrange("p u c e -> p (u c) e"),
                    in0=size_acc[g, c0, u0][:].rearrange("p e u c -> p (u c) e"),
                    scalar=0.0,
                    in1=pos_energy[g, c0][:, u0 : u0 + pairs, :, :].rearrange("p u c e -> p (u c) e"),
                    op0=ALU.max,
                    op1=ALU.mult,
                )

        def root(g, chunk):
            c0, width = chunk
            h_bf[g, c0] = held([P, 4 * width], BF16, "h_bf%d_%d" % (g, c0))
            nc.scalar.activation(
                h_bf[g, c0][:].rearrange("p (c u e) -> p c u e", u=2, e=2),
                prod[g, c0][:].rearrange("p u c e -> p c u e"),
                ACT.Sqrt,
            )

        def quantise_h(g, chunk):
            c0, width = chunk
            h_w[g, c0] = held([P, width], U32, "h_w%d_%d" % (g, c0))
            h_sc[g, c0] = held([P, width], U8, "h_sc%d_%d" % (g, c0))
            nc.vector.quantize_mx(out=h_w[g, c0][:].bitcast(FP8X4), scales=h_sc[g, c0][:], in_=h_bf[g, c0][:])

        late = {}

        def deal_wi():
            late["wi_w"] = held([P, 2, N], I32, "wi_w", round_tags[1])
            late["bias"] = held([P, 4], F32, "bias", "picked_sc")
            nc.sync.dma_start(late["bias"][:], b.rearrange("(p t) -> p t", t=4))
            nc.scalar.copy(
                late["wi_w"][:].bitcast(U32).rearrange("p a (t m) -> p a m t", t=4),
                wi_raw[:].bitcast(U32).rearrange("p a (m t) -> p a m t", t=4),
            )

        y_sc = held([P, S], U8, "y_sc")
        y_w = held([P, S], I32, "y_w")
        y_rows = out_0.rearrange("(p t) j -> p t j", t=4)
        y_words = out_1[0].rearrange("p m i -> p (m i)").bitcast(I32)
        y, y_bf, last_acc = {}, {}, {}

        def interaction_pass(out, c0, t, g, opening):
            nc.tensor.matmul_mx(
                out=out,
                lhsT=late["wi_w"][:, g, P * t : P * (t + 1)].bitcast(FP8X4),
                lhsT_scale=wi_sc[g][:, P * t : P * (t + 1)],
                rhs=h_w[g, c0][:].bitcast(FP8X4),
                rhs_scale=h_sc[g, c0][:],
                start=(g == opening),
                stop=(g != opening),
            )

        def add_bias(c0, t, acc):
            nc.scalar.activation(y[c0][:, t, :], acc, ACT.Identity, bias=late["bias"][:, t : t + 1])

        def interactions(chunk):
            c0, width = chunk
            y[c0] = held([P, 4, width], F32, "y%d" % c0)
            for t0 in (0, 2):
                acc = bank([P, 2, width])
                for t in (t0, t0 + 1):
                    for g in (1, 0):
                        interaction_pass(acc[:, t - t0, :], c0, t, g, 1)
                if t0 == 2 and chunk == SHARED_CHUNK:
                    spread = late["bias"][:, 2:4].unsqueeze(2).to_broadcast([P, 2, width])
                    nc.vector.tensor_tensor(y[c0][:, 2:4, :], acc[:], spread, ALU.add)
                else:
                    for t in (t0, t0 + 1):
                        add_bias(c0, t, acc[:, t - t0, :])
            nc.sync.dma_start(y_rows[:, :, c0 : c0 + width], y[c0][:])

        def open_last(chunk):
            c0, width = chunk
            for t in range(4):
                last_acc[t] = bank([P, width])
                interaction_pass(last_acc[t][:], c0, t, 0, 0)

        def close_last(chunk):
            c0, width = chunk
            y[c0] = held([P, 4, width], F32, "y%d" % c0)
            for t in range(4):
                interaction_pass(last_acc[t][:], c0, t, 1, 0)
                if t % 2 == 0:
                    add_bias(c0, t, last_acc[t][:])
                else:
                    nc.vector.tensor_scalar(
                        out=y[c0][:, t, :],
                        in0=last_acc[t][:],
                        scalar1=late["bias"][:, t : t + 1],
                        scalar2=None,
                        op0=ALU.add,
                    )
            nc.sync.dma_start(y_rows[:, :, c0 : c0 + width], y[c0][:])

        def round_y(chunk):
            c0, width = chunk
            y_bf[c0] = held([P, 4 * width], BF16, "y_bf%d" % c0)
            nc.vector.tensor_copy(
                y_bf[c0][:].rearrange("p (c i t) -> p c t i", i=2, t=4),
                y[c0][:].rearrange("p t (c i) -> p c t i", i=2),
            )

        def quantise_y(chunk):
            c0, width = chunk
            end = c0 + width
            nc.vector.quantize_mx(out=y_w[:, c0:end].bitcast(FP8X4), scales=y_sc[:, c0:end], in_=y_bf[c0][:])
            if end in WORD_STORES:
                nc.sync.dma_start(y_words[:, WORD_STORES[end] : end], y_w[:, WORD_STORES[end] : end])

        banks = [(c0, u) for c0 in range(0, S, QUARTER) for u in range(2)]
        for a in range(2):
            for c0, u in banks:
                energy_pass(0, c0, u, a, 0)

        round_ws(0, 0)
        quantise_ws(0, 0)
        energy_banks(1, banks[:5])
        round_ws(1, 0)
        quantise_ws(1, 0)
        round_ws(0, 1)
        size(*STEPS[0])
        size(*STEPS[1])
        energy_banks(1, banks[5:])
        size(*STEPS[2])
        product(*STEPS[0])
        root(*STEPS[0])
        quantise_ws(0, 1)
        round_ws(1, 1)
        product(*STEPS[1])
        root(*STEPS[1])
        quantise_ws(1, 1)

        begun = 2
        for step in STEPS[begun + 1 : begun + AHEAD]:
            size(*step)
        for i in range(begun, len(STEPS) + 1):
            if i + AHEAD < len(STEPS):
                size(*STEPS[i + AHEAD])
            if i < len(STEPS):
                product(*STEPS[i])
            if i == begun:
                deal_wi()
            g, chunk = STEPS[i - 1]
            if g == 1:
                if chunk == CHUNKS[1]:
                    round_y(CHUNKS[0])
                quantise_h(0, chunk)
                if chunk == CHUNKS[1]:
                    quantise_y(CHUNKS[0])
                if chunk == CHUNKS[-1]:
                    open_last(chunk)
                    quantise_h(1, chunk)
                    close_last(chunk)
                else:
                    quantise_h(1, chunk)
                    interactions(chunk)
            if i < len(STEPS):
                root(*STEPS[i])

        round_y(CHUNKS[1])
        for chunk, following in zip(CHUNKS[1:], CHUNKS[2:] + [None]):
            if following:
                round_y(following)
            quantise_y(chunk)
        for q in range(4):
            queue = nc.scalar if q % 2 else nc.sync
            queue.dma_start(out_2[0, 4 * q : 4 * q + 4, :].bitcast(I32), y_sc[32 * q : 32 * q + 4, :].bitcast(I32))
